import numpy as np, ml_dtypes
CORES = [3,7,11,15,131,135,139,143]
N = 8
BF = ml_dtypes.bfloat16
L, WX, W, FD, RO = 256, 4096, 1024, 64, 3
LW = 10
WT = 2 * np.arange(16) + 1
KINDS = np.array([[16, 0, 0, 0], [15, 1, 0, 0], [8, 8, 0, 0], [4, 4, 4, 4], [13, 1, 1, 1], [7, 6, 2, 1], [14, 2, 0, 0], [6, 5, 5, 0]])
SEQ = np.stack([np.repeat(np.arange(4), a) for a in KINDS])
def move(a):
    return np.ascontiguousarray(a.reshape(N, 8, 16, N, L // N).transpose(3, 1, 2, 0, 4)).reshape(N, 8, 16, L)
def pack(X, C, M, S, Z):
    return {"x0": np.ascontiguousarray(X.reshape(N, 128, WX)).astype(np.float32).astype(BF), "cm": np.ascontiguousarray((W * M + C).reshape(N, 128, W)).astype(np.int32),
            "s0": np.ascontiguousarray(S.reshape(N, 128, L)).astype(np.int32), "z0": np.ascontiguousarray(Z.reshape(N, 128, L)).astype(np.float32).astype(BF)}
def parts(rng):
    X = rng.integers(0, 256, (N, 8, 16, WX)); C = rng.integers(0, W, (N, 8, 16, W)); M = rng.integers(0, W, (N, 8, 16, W))
    share = rng.choice(np.array([0.1, 0.3, 0.6]), (N, 8, 1, 1)); pool = rng.integers(0, W, (N, 8, 1, 64))
    few = np.take_along_axis(pool, rng.integers(0, 64, (N, 8, 1, 16 * W)), 3).reshape(N, 8, 16, W)
    C = np.where(rng.random(C.shape) < share, few, C)
    return X, C, M, rng.integers(0, W, (N, 8, 16, L)), rng.integers(0, 256, (N, 8, 16, L))
def classes(rng, kinds):
    s = np.take_along_axis(np.argsort(rng.random((L, 4)), axis=1), SEQ[kinds], 1)
    return np.take_along_axis(s, np.argsort(rng.random((L, 16)), axis=1), 1).T
def juries(rng, X, C, S, Z, q, g, cl):
    v = rng.permutation(W); off = rng.integers(0, W, 16); kind = int(rng.integers(0, 4))
    C[q, g] = v[(np.arange(W)[None, :] + off[:, None]) % W]
    base = np.zeros(16, np.int64) if kind == 0 else np.full(16, 255) if kind == 1 else rng.integers(0, 256, 16)
    Z[q, g] = base[np.argsort(rng.random((16, L)), axis=0)]
    u = int(np.add.reduce(base)); h = (((v * (u + 1)) >> 5) + v) & (WX - 1)
    b = np.add.reduce(X[q, g][:, h] * WT[:, None], axis=0) & 3
    start = rng.integers(0, W, (1, L))
    for c in range(4):
        m = (cl == c).astype(np.int64); before = np.add.accumulate(m, axis=0) - m
        pl = np.flatnonzero(b == c)
        if len(pl) == 0: pl = np.arange(W)
        S[q, g] = np.where(m == 1, (pl[(start + before) % len(pl)] - off[:, None]) % W, S[q, g])
    return off
def setup_inputs(rng):
    return pack(*parts(rng))
def setup_inputs_spread(rng):
    def uneven(n, hi, *shape):
        return np.minimum((hi * rng.random((N, 8, 16, n)) ** rng.choice(np.array([0.125, 0.5, 1.0, 2.0, 5.0]), shape)).astype(np.int64), hi - 1)
    return pack(uneven(WX, 256, N, 8, 1, WX), uneven(W, W, N, 8, 1, 1), uneven(W, W, N, 8, 16, 1), uneven(L, W, N, 8, 1, L), uneven(L, 256, N, 8, 1, L))
def setup_inputs_ends(rng):
    p = np.array([0.0, 0.1, 0.5, 0.9, 1.0])
    X = 255 * (rng.random((N, 8, 16, WX)) < rng.choice(p, (N, 8, 1, WX))).astype(np.int64)
    C = (W - 1) * rng.integers(0, 2, (N, 8, 16, W)); S = (W - 1) * rng.integers(0, 2, (N, 8, 16, L))
    Z = 255 * (rng.random((N, 8, 16, L)) < rng.choice(p, (N, 8, 1, L))).astype(np.int64)
    Z[..., L - 1] = 255; Z[..., 0] = 255; Z[..., 1] = 0; Z[..., L - 2] = 0
    C[:, :, 15, W - 1] = W - 1; S[:, :, 15, L - 1] = W - 1; S[:, :, 15, 0] = W - 1
    X[:, 0] = X[:, 0, :1]
    X[:, :, :, WX - 1] = 255; X[:, ::2, :, 0] = 255; X[:, 1::2, :, 0] = 0
    C[:, 7, :, W - 1] = W - 1; S[:, 7, :, L - 1] = W - 1; S[:, 7, :, 2] = W - 1
    C[:, 5, :, 0] = 0; C[:, 5, :, W - 1] = W - 1
    S[:, 5] = (W - 1) * (np.arange(16)[:, None] == rng.integers(0, 16, (N, 1, L)))
    Z[:, 5] = np.where(Z[:, 5, :1] > 0, 255, 0)
    X[:, 5, :, (613 * np.arange(15)) & (WX - 1)] = 0
    for u in (0, 4080):
        h = ((((W - 1) * (u + 1)) >> 5) + W - 1) & (WX - 1)
        X[:, 5, :, h] = 0; X[:, 5, 0, h] = 255
    M = np.where(rng.random(C.shape) < 0.8, C, W - 1 - C)
    return pack(X, C, M, S, Z)
def setup_inputs_corners(rng):
    X, C, M, S, Z = parts(rng)
    for q in range(N):
        for g in range(8):
            off = juries(rng, X, C, S, Z, q, g, classes(rng, rng.integers(0, 8, L)))
            w = rng.random(L); c = rng.integers(0, W, L)
            S[q, g] = np.where((w < 0.15)[None, :], (c[None, :] - off[:, None]) % W, S[q, g])
            S[q, g, 15] = np.where(w > 0.8, (S[q, g, 0] + off[0] - off[15]) % W, S[q, g, 15])
    return pack(X, C, M, S, Z)
def setup_inputs_crowd(rng):
    X, C, M, S, Z = parts(rng)
    for q in range(N):
        for g in range(8):
            w = (g + q) % 8; kinds = np.full(L, (1, 1, 0, 5, 5, 6, 3, 4)[w]); one = int(rng.integers(0, L))
            if w == 1: kinds[one] = 0
            off = juries(rng, X, C, S, Z, q, g, classes(rng, kinds))
            if w == 3: S[q, g] = S[q, g, :, :1].copy()
            if w == 4: S[q, g] = ((int(rng.integers(0, W)) - off) % W)[:, None]
            if w == 5:
                mine = S[q, g, :, one].copy(); S[q, g] = S[q, g, :, (one + 1) % L].copy()[:, None]; S[q, g, :, one] = mine
    return pack(X, C, M, S, Z)
def setup_inputs_tops(rng):
    X, C, M, S, Z = parts(rng)
    X[:, 1::2] = 255 - (rng.random((N, 4, 16, WX)) < 0.25).astype(np.int64)
    C = np.where(rng.random(C.shape) < 0.5, rng.choice(np.array([W - 17, W - 5, W - 3, W - 1]), C.shape), rng.integers(W - 96, W, C.shape))
    lack = rng.integers(0, 17, (N, 8, 1, L)); lack[..., 0::4] = 4; lack[..., 1::4] = 6; lack[..., 2::4] = 0; lack[..., L - 1] = 4
    Z = 255 - (np.argsort(rng.random((N, 8, 16, L)), axis=2) < lack).astype(np.int64)
    C[:, :, 15, W - 1] = W - 5; S[:, :, 15, L - 1] = W - 1
    return pack(X, C, M, S, Z)
def check_inputs(d):
    bad = []
    for k, hi in (("x0", 255), ("cm", W * W - 1), ("s0", W - 1), ("z0", 255)):
        a = np.asarray(d[k]).astype(np.float64)
        if not (np.min(a) >= 0 and np.max(a) <= hi): bad.append("range of " + k)
        elif np.any(a != np.floor(a)): bad.append("whole numbers in " + k)
    return bad
def reference(x0, cm, s0, z0):
    X = x0.astype(np.float32).astype(np.int64).reshape(N, 8, 16, WX); both = cm.astype(np.int64).reshape(N, 8, 16, W)
    C = both & (W - 1); M = both >> LW
    S = s0.astype(np.int64).reshape(N, 8, 16, L); Z = z0.astype(np.float32).astype(np.int64).reshape(N, 8, 16, L)
    A = np.zeros((N, 8, 1, 1), np.int64); k = np.arange(16); lane = np.arange(L); less = (k[:, None] > k[None, :])[:, :, None]
    for t in range(RO):
        e = np.take_along_axis(C[:, :, (k + t) & 15], S, 3)
        same = (e[:, :, :, None, :] == e[:, :, None, :, :]) & less
        o = np.add.reduce(same.astype(np.int64), axis=3)
        u = np.add.reduce(Z, axis=2)[:, :, None, :]
        h = (((e * (u + 1)) >> 5) + e + 613 * o + A) & (WX - 1)
        x = np.take_along_axis(X, h.reshape(N, 8, 1, 16 * L), 3).reshape(N, 8, 16, 16, L)
        b = np.add.reduce(x * WT[:, None, None], axis=2) & 3
        count = np.stack([np.add.reduce((b == c).astype(np.int64), axis=2) for c in range(4)], axis=2)
        best = np.argmin(np.where(count == 0, 99, count), axis=2)[:, :, None, :]
        sv = b == best; si = sv.astype(np.int64)
        ns = np.add.reduce(si, axis=2)[:, :, None, :]; before = np.add.accumulate(si, axis=2) - si
        place = np.where(sv, before, ns + k[:, None] - before)
        order = np.zeros_like(e); np.put_along_axis(order, place, e, 2)
        first = np.argmax(sv, axis=2)[:, :, None, :]
        hf = np.take_along_axis(h, first, 2); xf = np.take_along_axis(x, first[:, :, None], 3)[:, :, :, 0]
        y = np.take_along_axis(M, e.reshape(N, 8, 1, 16 * L), 3).reshape(N, 8, 16, 16, L)
        Z = np.maximum.reduce(np.where(sv[:, :, None], x, 0), axis=3)
        S = np.maximum.reduce(np.where(sv[:, :, None], y, 0), axis=3)
        np.put_along_axis(C, np.broadcast_to((W // L) * lane + (u & (W // L - 1)), (N, 8, 16, L)), order, 3)
        np.put_along_axis(X, np.broadcast_to(hf - (hf & (L - 1)) + lane, (N, 8, 16, L)), (xf + Z) >> 1, 3)
        A = np.add.reduce((ns == 1).astype(np.int64), axis=3)[..., None]
        if t < RO - 1:
            S = move(S); Z = move(Z)
    yx = np.add.reduce(X.reshape(N, 128, WX // FD, FD) * np.arange(1, WX // FD + 1)[:, None], axis=2)
    yc = np.add.reduce(C.reshape(N, 128, W // FD, FD) * np.arange(1, W // FD + 1)[:, None], axis=2)
    return {"yx": yx.astype(np.float32), "yc": yc.astype(np.float32), "ys": np.ascontiguousarray(S).reshape(N, 128, L).astype(np.float32), "yz": np.ascontiguousarray(Z).reshape(N, 128, L).astype(np.float32).astype(BF)}

@@ -1,0 +1,515 @@
+from concourse.bass import DstId, RemoteDMATransfer
+from concourse.mybir import dt, AluOpType, AxisListType, ActivationFunctionType
+
+A = AluOpType
+AF = ActivationFunctionType
+LEVELS = 3
+
+_B, _H, _F, _I, _U = "bfloat16", "float16", "float32", "int32", "uint16"
+PACK, _w = {}, {}
+for _b, _n, _c in [("B7", x, 128) for x in ("VK", "SV", "AL", "PR", "TP", "SVL", "VM")] + [
+        ("IS", "UI", 16), ("IS", "KI", 32), ("IS", "KJ", 24), ("IS", "BN", 16), ("IS", "VI", 8), ("IS", "R", 24)]:
+    PACK[_n] = (_b, _w.get(_b, 0), _c)
+    _w[_b] = _w.get(_b, 0) + _c
+KP = {_n: 128 * _i for _i, _n in enumerate(("KM7", "KM2", "KC16", "NI", "I2"))}
+SCRATCH = {
+    "XW": ("sbuf", [128, 4096], _B), "CM": ("sbuf", [128, 1024], _I), "CW": ("sbuf", [128, 1024], _I),
+    "MW": ("sbuf", [128, 1024], _I), "S3": ("sbuf", [128, 8, 2, 16], _I), "Z3": ("sbuf", [128, 8, 2, 16], _B),
+    "CF": ("sbuf", [128, 1024], _H),
+    "ON2": ("sbuf", [128, 128], _B), "ON3": ("sbuf", [128, 8, 8, 16], _B), "ID": ("sbuf", [128, 128], _B),
+    "ID3": ("sbuf", [128, 8, 16], _B), "BO": ("sbuf", [128, 8, 16], _B), "WB": ("sbuf", [128, 8], _B),
+    "LS": ("sbuf", [128, 8, 8, 16], _B), "DG": ("sbuf", [128, 64], _B), "FQ": ("sbuf", [128, 4, 8, 16], _B),
+    "BK": ("sbuf", [128, 16, 8, 16], _B), "I613": ("sbuf", [128, 128], _H), "KP": ("sbuf", [128, 640], _B),
+    "RM": ("sbuf", [128, 512], _B), "RM8": ("sbuf", [128, 64], _B), "KCC": ("sbuf", [128, 32], _B),
+    "MUL": ("sbuf", [128, 24], _I), "AD0": ("sbuf", [128, 24], _I), "AD1": ("sbuf", [128, 24], _I),
+    "BS0": ("sbuf", [128, 24], _I), "BS1": ("sbuf", [128, 24], _I), "QI": ("sbuf", [128, 16], _I),
+    "QJ": ("sbuf", [128, 16], _I), "QC": ("sbuf", [128, 16], _F), "RA": ("sbuf", [128, 16], _F), "RB": ("sbuf", [128, 16], _F),
+    "DI": ("sbuf", [128, 64, 128], _B),
+    "OS": ("sbuf", [128, 8, 2, 16], _F), "OZ": ("sbuf", [128, 8, 2, 16], _B),
+    "OX": ("sbuf", [128, 64], _F), "OC": ("sbuf", [128, 64], _F),
+    "D0": ("psum", [128, 512], _F), "D1": ("psum", [128, 512], _F),
+}
+for _c in "01":
+    SCRATCH.update({
+        "E" + _c: ("psum", [128, 4, 8, 16], _F), "Q" + _c: ("psum", [128, 4, 8, 16], _F),
+        "L" + _c: ("psum", [128, 512], _F),
+        "B7" + _c: ("sbuf", [128, _w["B7"]], _B), "IS" + _c: ("sbuf", [128, _w["IS"]], _I),
+        "ZC" + _c: ("sbuf", [128, 128], _H), "OFS" + _c: ("sbuf", [128, 128], _U), "OFM" + _c: ("sbuf", [128, 128], _U),
+        "OFX" + _c: ("sbuf", [128, 128], _U), "CG" + _c: ("sbuf", [128, 2048], _H), "YG" + _c: ("sbuf", [128, 2048], _H),
+        "XG" + _c: ("sbuf", [128, 2048], _B), "XS" + _c: ("sbuf", [128, 2048], _H), "YS" + _c: ("sbuf", [128, 2048], _H),
+        "ES" + _c: ("sbuf", [128, 8, 16], _H), "EQ" + _c: ("sbuf", [128, 15, 8, 16], _B),
+        "U1" + _c: ("sbuf", [128, 8, 16], _F), "U3" + _c: ("sbuf", [128, 8], _F),
+        "WI" + _c: ("sbuf", [128, 8, 16], _I), "HI" + _c: ("sbuf", [128, 8, 16], _I), "H8" + _c: ("sbuf", [128, 8, 16], _I),
+        "HF" + _c: ("sbuf", [128, 8, 16], _H), "BI" + _c: ("sbuf", [128, 128], _I),
+        "IN" + _c: ("sbuf", [128, 512], _B), "CT" + _c: ("sbuf", [128, 512], _B), "KB" + _c: ("sbuf", [128, 256], _B),
+        "BB" + _c: ("sbuf", [128, 256], _B),
+        "TT" + _c: ("sbuf", [128, 8, 3, 16], _H), "TL" + _c: ("sbuf", [128, 4, 8, 16], _H),
+        "FR" + _c: ("sbuf", [128, 4, 4, 8, 16], _H), "FC" + _c: ("sbuf", [128, 128], _F), "O1" + _c: ("sbuf", [128, 8, 16], _B),
+        "VT" + _c: ("sbuf", [128, 8], _H), "LM" + _c: ("sbuf", [128, 64], _H), "LV" + _c: ("sbuf", [128, 64], _H),
+        "LST" + _c: ("sbuf", [128, 24], _U), "NZ" + _c: ("sbuf", [128, 128], _H),
+        "XQ" + _c: ("sbuf", [128, 128], _I), "XR" + _c: ("sbuf", [128, 128], _I), "DS" + _c: ("sbuf", [128, 2048], _B),
+        "SZ0" + _c: ("sbuf", [128, 8, 32], _H), "SZ1" + _c: ("sbuf", [128, 8, 32], _H),
+        "RZ0" + _c: ("sbuf", [128, 8, 32], _H), "RZ1" + _c: ("sbuf", [128, 8, 32], _H),
+    })
+SEMAPHORES = ["V", "S", "P", "G", "ds", "dz", "dc", "dx", "os", "oz", "ox", "oc"] + [
+    k + t + c for k in ("arr", "snt") for t in "01" for c in "01"]
+
+
+def calls_of(src, cores, topo):
+    here = [c for c in topo.cores_of(src) if c in cores and c != src]
+    off = [c for c in cores if c != src and c not in here]
+    off.sort(key=lambda c: (2 if topo.mates(src, c) else 1 if topo.same_plane(src, c) else 0, c))
+    eng = topo.engines(src, off[0])
+    half = len(off) - 2
+    w = len(eng) // half
+    first = [(d, eng[w * i:w * i + w]) for i, d in enumerate(off[:half])]
+    w = len(eng) // 2
+    second = [(d, eng[w * i:w * i + w]) for i, d in enumerate(off[half:])]
+    for d in here:
+        second.append((d, [e for e in topo.engines(src, d) if e not in eng]))
+    return [first, second]
+
+
+def rank_program(g, core, T, topo):
+    rank = T.rank_of(core)
+    if rank is None:
+        return
+    cores = list(T.cores)
+    E = {"V": g.vector, "S": g.scalar, "P": g.tensor, "G": g, "Y": g.sync}
+    cnt, known = {}, {e: {} for e in E}
+    wr, rd, bank = {}, {}, {}
+
+    def sync(e, R, W, B):
+        need = {}
+        toks = [wr[r] for r in list(R) + list(W) if r in wr]
+        for w in W:
+            toks += list(rd.get(w, {}).values())
+        for b in B:
+            toks += [t for f, t in bank.get(b, {}).items() if f != e]
+        for t in toks:
+            if t[0] not in need or need[t[0]][1] < t[1]:
+                need[t[0]] = t
+        for sem in sorted(need, key=lambda x: x == e):
+            sm, val, clk = need[sem]
+            if known[e].get(sm, 0) < val:
+                E[e].wait_ge(T.sem[sm], val)
+                for k2, v2 in clk.items():
+                    known[e][k2] = max(known[e].get(k2, 0), v2)
+                known[e][sm] = val
+
+    def note(e, tok, R, W, B):
+        for w in W:
+            wr[w] = tok
+            rd[w] = {}
+        for r in R:
+            rd.setdefault(r, {})[tok[0]] = tok
+        for b in B:
+            bank.setdefault(b, {})[e] = tok
+
+    def op(e, R, W, B, f):
+        sync(e, R, W, B)
+        ins = f()
+        for i in (ins if isinstance(ins, list) else [ins]):
+            i.then_inc(T.sem[e], 1)
+            cnt[e] = cnt.get(e, 0) + 1
+        note(e, (e, cnt[e], dict(known[e])), R, W, B)
+
+    def dma(e, sem, out, in_, R, W):
+        sync(e, R, W, [])
+        E[e].dma_start(out, in_).then_inc(T.sem[sem], 16)
+        cnt[sem] = cnt.get(sem, 0) + 16
+        note(e, (sem, cnt[sem], dict(known[e])), R, W, [])
+
+    v, s, p = g.vector, g.scalar, g.tensor
+
+    def copy(out, in_, R, W, B=()):
+        op("V", R, W, B, lambda: v.tensor_copy(out, in_))
+
+    def ts(out, in0, s1, op0, R, W, B=(), s2=None, op1=None):
+        if op1 is None:
+            op("V", R, W, B, lambda: v.tensor_scalar(out, in0, s1, None, op0))
+        else:
+            op("V", R, W, B, lambda: v.tensor_scalar(out, in0, s1, s2, op0, op1))
+
+    def tt(out, a, b, o, R, W, B=()):
+        op("V", R, W, B, lambda: v.tensor_tensor(out, a, b, o))
+
+    def scan(out, a, b, ini, o0, o1, R, W, B=()):
+        op("V", R, W, B, lambda: v.tensor_tensor_scan(out, a, b, ini, o0, o1))
+
+    def fill(ap, x, W):
+        op("V", [], W, [], lambda: v.memset(ap, x))
+
+    def iota(out, pat, base, cm, W, small=True):
+        op("G", [], W, [], lambda: g.iota(out, pat, base, cm, allow_small_or_imprecise_dtypes=True) if small
+           else g.iota(out, pat, base, cm))
+
+    def sel(out, in_, pat, cmp, fl, base, cm, R, W):
+        op("G", R, W, [], lambda: g.affine_select(out, in_, pat, cmp, fl, base, cm))
+
+    def X(name, c):
+        return T[name + str(c)]
+
+    def K(name, c, a=0, b=None, st=1):
+        buf, off, w = PACK[name]
+        return T[buf + str(c)][:, off + a:off + (w if b is None else b):st]
+
+    def C(name):
+        return T.KP[:, KP[name]:KP[name] + 128]
+
+    dma("S", "dc", T.CM[:], T.cm[:], [], ["CM"])
+    dma("Y", "ds", T.S3[:], T.s0[:], [], ["S3"])
+    dma("Y", "dz", T.Z3[:], T.z0[:], [], ["Z3"])
+    dma("Y", "dx", T.XW[:], T.x0[:], [], ["XW"])
+    fill(T.ON2[:], 1.0, ["ON2"])
+    fill(T.ON3[:], 1.0, ["ON3"])
+    iota(T.QI[:], [[-1, 16]], 0, 1, ["QI"], False)
+    sel(T.ID[:], T.ON2[:], [[-1, 128]], A.is_equal, 0.0, 0, 1, ["ON2"], ["ID"])
+    sel(T.BO[:], T.ON3[:, 0], [[-16, 8], [0, 16]], A.is_ge, 0.0, 0, 1, ["ON3"], ["BO"])
+    sel(T.BO[:], T.BO[:], [[16, 8], [0, 16]], A.is_ge, 0.0, 15, -1, ["BO"], ["BO"])
+    iota(C("KC16"), [[0, 8], [-16, 16]], 240, 0, ["KC16"])
+    iota(T.KCC[:], [[1, 4], [0, 8]], -4, 0, ["KCC"])
+    iota(C("KM7"), [[0, 8], [1, 16]], -7, 0, ["KM7"])
+    iota(C("KM2"), [[0, 8], [-1, 16]], -2, 0, ["KM2"])
+    sel(T.LS[:], T.ON3[:], [[-16, 8], [0, 8], [-1, 16]], A.is_equal, 0.0, 0, 1, ["ON3"], ["LS"])
+    sel(T.DG[:], T.ON2[:, 0:64], [[0, 8], [-16, 8]], A.is_ge, 0.0, 0, 1, ["ON2"], ["DG"])
+    sel(T.DG[:], T.DG[:], [[0, 8], [16, 8]], A.is_ge, 0.0, 15, -1, ["DG"], ["DG"])
+    for c in (0, 1):
+        bs = X("BS", c)
+        iota(bs[:, 0:8], [[32, 8]], 16 * c, 0, ["BS%da" % c], False)
+        iota(bs[:, 8:16], [[128, 8]], 64 * c, 0, ["BS%db" % c], False)
+        iota(bs[:, 16:24], [[256, 8]], 15, 0, ["BS%dc" % c], False)
+    iota(T.FQ[:], [[0, 4], [0, 8], [2048, 16]], -16384, 0, ["FQ"])
+    sel(T.FQ[:], T.FQ[:], [[-1, 4], [-12, 8], [0, 16]], A.is_equal, 0.0, -4, 1, ["FQ"], ["FQ"])
+    sel(T.FQ[:], T.FQ[:], [[-1, 4], [-12, 8], [0, 16]], A.not_equal, 1.0, 0, 1, ["FQ"], ["FQ"])
+    sel(T.FQ[:], T.FQ[:], [[-1, 4], [-12, 8], [0, 16]], A.not_equal, -1024.0, -8, 1, ["FQ"], ["FQ"])
+    ts(T.QJ[:], T.QI[:], 15, A.bitwise_and, ["QI"], ["QJ"])
+    q = T.QC
+    copy(q[:, 0:1], T.QJ[:, 0:1], ["QJ"], ["q0"])
+    fill(T.RM[:], 1.0, ["RM"])
+    ts(q[:, 1:2], q[:, 0:1], 2.0, A.mult, ["q0"], ["q1"], (), 1.0, A.add)
+    ts(q[:, 2:3], q[:, 0:1], 4.0, A.mult, ["q0"], ["q2"])
+    ts(q[:, 3:4], q[:, 0:1], 16.0, A.mult, ["q0"], ["q3"])
+    ts(q[:, 4:5], q[:, 0:1], -8.0, A.add, ["q0"], ["q4"])
+    ts(T.RA[:], T.QJ[:], 0, A.is_equal, ["QJ"], ["RA"], (), 1024.0, A.mult)
+    ts(T.RB[:], T.QJ[:], 1, A.is_equal, ["QJ"], ["RB"], (), 1024.0, A.mult)
+    tt(q[:, 5:6], q[:, 4:5], q[:, 4:5], A.mult, ["q4"], ["q5"])
+    tt(T.RA[:, 0:15], T.RA[:, 0:15], T.RB[:, 0:15], A.subtract, ["RA", "RB"], ["RA"])
+    ts(q[:, 6:7], q[:, 5:6], -1024.0, A.mult, ["q5"], ["q6"])
+    copy(T.ID3[:], T.ID[:], ["ID"], ["ID3"])
+    ts(T.I613[:], T.ID[:], 613.0, A.mult, ["ID"], ["I613"])
+    ts(C("NI"), T.ID[:], -1.0, A.mult, ["ID"], ["NI"])
+    ts(C("I2"), T.ID[:], 2.0, A.mult, ["ID"], ["I2"])
+    ts(T.WB[:], T.BO[:, :, 0], q[:, 1:2], A.mult, ["BO", "q1"], ["WB"])
+    fill(T.RM8[:], 1.0, ["RM8"])
+    fill(T.KB0[:], 0.0, ["KB0"])
+    fill(T.KB1[:], 0.0, ["KB1"])
+    fill(T.RM[:, ::16], 0.0, ["RM"])
+    fill(T.RM8[:, ::8], 0.0, ["RM8"])
+    fill(T.MUL[:, 0:8], 256, ["MULa"])
+    fill(T.MUL[:, 8:16], 1, ["MULb"])
+    fill(T.MUL[:, 16:24], -1, ["MULc"])
+    for k in range(16):
+        ts(T.BK[:, k], T.BO[:], T.RA[:, k:k + 1], A.mult, ["BO", "RA"], ["BK%d" % k])
+
+    def late_constants():
+        for c in (0, 1):
+            for j, n in ((0, 0), (1, 2), (2, 3)):
+                ts(X("AD", c)[:, 8 * j:8 * j + 8], X("BS", c)[:, 8 * j:8 * j + 8], q[:, n:n + 1], A.add,
+                   ["BS%d%s" % (c, "abc"[j]), "q%d" % n], ["AD%d%s" % (c, "abc"[j])])
+
+    def gather(e, out, win, off, R, W):
+        if e == "V":
+            op("V", R, W, [], lambda: v.tensor_copy(out, win.indirect(off)))
+        else:
+            op("S", R, W, [], lambda: s.activation(out, win.indirect(off), AF.Copy))
+
+    def seats(t, c):
+        n = str(c)
+        if t == 0:
+            copy(X("OFS", c)[:], T.S3[:, :, c, :], ["S3"], ["OFS" + n])
+        else:
+            key = "RZ%d%d" % (t - 1, c)
+            ts(X("OFS", c)[:], T[key][:, :, 0:16], 0.0, A.add, [key, key + "o"], ["OFS" + n])
+
+    def zrow(t, c):
+        n = str(c)
+        if t == 0:
+            copy(X("ZC", c)[:], T.Z3[:, :, c, :], ["Z3"], ["ZC" + n])
+        else:
+            key = "RZ%d%d" % (t - 1, c)
+            copy(X("ZC", c)[:], T[key][:, :, 16:32], [key, key + "o"], ["ZC" + n])
+        Eb = X("E", c)
+        op("P", ["ZC" + n, "BO"], [], ["E" + n], lambda: [
+            p.matmul(Eb[:, 1], X("ZC", c)[:], T.BO[:], True, True),
+            p.matmul(Eb[:, 2, :, 0], X("ZC", c)[:], T.BO[:, :, 0], True, True)])
+
+    def cgather(e, c, a, b):
+        n = str(c)
+        gather(e, X("CG", c)[:, 16 * a:16 * b], T.CW[:, 0:1024], X("OFS", c)[:, a:b], ["CW", "OFS" + n],
+               ["CG%d%s" % (c, "b" if a else "a")])
+
+    def members(t, c):
+        n = str(c)
+        op("P", ["CG" + n + "a", "CG" + n + "b", "ID"], [], ["E" + n], lambda: [
+            p.matmul(X("E", c)[:, 0, :, k], X("CG", c)[:, k::16], T.ID[:, (k + t) & 15::16], True, True) for k in range(16)])
+
+    def hashes(t, c):
+        n = str(c)
+        Eb, Qb, Lb = X("E", c), X("Q", c), X("L", c)
+        es, eq, u1, wi, hi = X("ES", c), X("EQ", c), X("U1", c), X("WI", c), X("HI", c)
+        EB = ["E" + n]
+        copy(es[:], Eb[:, 0], [], ["ES" + n], EB)
+        op("P", ["ES" + n, "ID"], [], ["L" + n], lambda: p.matmul(Lb[:, 0:128], es[:], T.ID[:], True, True))
+
+        def base():
+            r = [p.matmul(Qb[:, 0], T.ID[:], es[:], True, False)]
+            if t > 0:
+                r += [p.matmul(Qb[:, 0], T.ON2[:], X("O1", j)[:], False, False) for j in (0, 1)]
+            return r
+        op("P", ["ES" + n, "ID", "ON2", "O10", "O11"], [], ["Q" + n], base)
+        ts(u1[:], Eb[:, 1], 1.0, A.add, [], ["U1" + n], EB)
+
+        def equal(d):
+            tt(eq[:, d - 1, :, d:16], es[:, :, d:16], Eb[:, 0, :, 0:16 - d], A.is_equal, ["ES" + n], ["EQ%d_%d" % (c, d)], EB)
+            op("P", ["EQ%d_%d" % (c, d), "I613"], [], ["Q" + n],
+               lambda: p.matmul(Qb[:, 0, :, d:16], T.I613[:], eq[:, d - 1, :, d:16], False, d == 15))
+        equal(1)
+        equal(2)
+        copy(X("OFM", c)[:], Lb[:, 0:128], [], ["OFM" + n], ["L" + n])
+        tt(wi[:], u1[:], Eb[:, 0], A.mult, ["U1" + n], ["WI" + n], EB)
+        equal(3)
+        equal(4)
+        ts(wi[:], wi[:], 5, A.arith_shift_right, ["WI" + n], ["WI" + n])
+        copy(K("UI", c, 0, 8), Eb[:, 2, :, 0], [], ["UIa" + n], EB)
+        equal(5)
+        equal(6)
+        ts(K("UI", c, 8, 16), K("UI", c, 0, 8), 3, A.bitwise_and, ["UIa" + n], ["UIb" + n])
+        equal(7)
+        equal(8)
+        ts(X("U3", c)[:], K("UI", c, 8, 16), 256.0, A.mult, ["UIb" + n], ["U3" + n])
+        for d in range(9, 16):
+            equal(d)
+        copy(X("TT", c)[:, :, 0, :], es[:], ["ES" + n], ["TTa" + n])
+        tt(hi[:], wi[:], Qb[:, 0], A.add, ["WI" + n], ["HI" + n], ["Q" + n])
+        ts(hi[:], hi[:], 4095, A.bitwise_and, ["HI" + n], ["HI" + n])
+        ts(X("HF", c)[:], hi[:], -2048.0, A.add, ["HI" + n], ["HF" + n])
+        op("P", ["HF" + n, "ID"], [], ["L" + n], lambda: p.matmul(Lb[:, 0:128], X("HF", c)[:], T.ID[:], True, True))
+        ts(X("H8", c)[:], hi[:], 8, A.arith_shift_right, ["HI" + n], ["H8" + n])
+        ts(X("OFX", c)[:], Lb[:, 0:128], 2048.0, A.add, [], ["OFX" + n], ["L" + n])
+        tt(K("VK", c), X("H8", c)[:], C("KC16"), A.add, ["H8" + n, "KC16"], ["VK" + n])
+
+    def mgather(e, c):
+        n = str(c)
+        gather(e, X("YG", c)[:], T.MW[:, 0:1024], X("OFM", c)[:, 0:128], ["MW", "OFM" + n], ["YG" + n])
+
+    def xgather(e, c):
+        n = str(c)
+        gather(e, X("XG", c)[:], T.XW[:, 0:4096], X("OFX", c)[:, 0:128], ["XW", "OFX" + n], ["XG" + n])
+
+    def survivors(t, c):
+        n = str(c)
+        Lb, LB = X("L", c), ["L" + n]
+        xg, bi, ind = X("XG", c), X("BI", c), X("IN", c)
+        op("P", ["XG" + n, "WB"], [], LB, lambda: [
+            p.matmul(Lb[:, 128 + k:256:16], xg[:, k::16], T.WB[:], True, True) for k in range(16)])
+        copy(bi[:], Lb[:, 128:256], [], ["BI" + n], LB)
+        ts(bi[:], bi[:], 3, A.bitwise_and, ["BI" + n], ["BI" + n])
+        ink = ["IN%d_%d" % (c, b) for b in range(4)]
+        for b in range(4):
+            ts(ind[:, 128 * b:128 * b + 128], bi[:], b, A.is_equal, ["BI" + n], [ink[b]], (), 4.0, A.mult)
+        scan(X("CT", c)[:], T.RM[:], ind[:], 0.0, A.mult, A.add, ["RM"] + ink, ["CT" + n])
+        tt(K("KI", c), X("CT", c)[:, 15::16], T.KCC[:], A.add, ["CT" + n, "KCC"], ["KI" + n])
+        ts(K("KI", c), K("KI", c), 127, A.bitwise_and, ["KI" + n], ["KI" + n])
+        tt(K("KJ", c, 0, 16), K("KI", c, 0, 16), K("KI", c, 16, 32), A.min, ["KI" + n], ["KJ" + n])
+        tt(K("KJ", c, 16, 24), K("KJ", c, 0, 8), K("KJ", c, 8, 16), A.min, ["KJ" + n], ["KK" + n])
+        ts(K("BN", c, 0, 8), K("KJ", c, 16, 24), 3, A.bitwise_and, ["KK" + n], ["BNa" + n])
+        ts(K("BN", c, 8, 16), K("KJ", c, 16, 24), 2, A.arith_shift_right, ["KK" + n], ["BNb" + n])
+        copy(X("KB", c)[:, ::16], K("BN", c), ["BNa" + n, "BNb" + n], ["KB" + n])
+        scan(X("BB", c)[:], T.RM[:, 0:256], X("KB", c)[:], 0.0, A.mult, A.add, ["RM", "KB" + n], ["BB" + n])
+        tt(K("SV", c), bi[:], X("BB", c)[:, 0:128], A.is_equal, ["BI" + n, "BB" + n], ["SV" + n])
+        op("P", ["SV" + n, "ID"], [], LB, lambda: p.matmul(Lb[:, 0:128], K("SV", c), T.ID[:], True, True))
+        scan(K("PR", c), T.RM[:, 0:128], K("SV", c), 0.0, A.mult, A.add, ["RM", "SV" + n], ["PR" + n])
+        ts(K("AL", c), Lb[:, 0:128], -2.0, A.add, [], ["AL" + n], LB)
+
+    def spread(c):
+        n = str(c)
+        bks = ["BK%d" % k for k in range(16)]
+        for m in range(4):
+            D, db = T["D%d" % (m & 1)], "D%d" % (m & 1)
+            op("P", ["AL" + n] + bks, [], [db], lambda: [
+                p.matmul(D[:, 128 * j:128 * j + 128], T.BK[:, 4 * m + j], K("AL", c), True, True) for j in range(4)])
+            op("S", [], ["DS%d_%d" % (c, m)], [db], lambda: [
+                s.activation(X("DS", c)[:, 4 * m + j::16], D[:, 128 * j:128 * j + 128], AF.Copy) for j in range(4)])
+
+    def places(t, c):
+        n = str(c)
+        Lb, LB = X("L", c), ["L" + n]
+        bb, TTb = X("BB", c), X("TT", c)
+        op("P", ["PR" + n, "BB" + n, "ID", "NI", "I2", "KM7", "KM2"], [], LB, lambda: [
+            p.matmul(Lb[:, 384:512], T.ID[:], bb[:, 128:256], True, False),
+            p.matmul(Lb[:, 384:512], T.ID[:], C("KM7"), False, False),
+            p.matmul(Lb[:, 384:512], C("NI"), K("PR", c), False, True),
+            p.matmul(Lb[:, 256:384], C("NI"), bb[:, 128:256], True, False),
+            p.matmul(Lb[:, 256:384], T.ID[:], C("KM2"), False, False),
+            p.matmul(Lb[:, 256:384], C("I2"), K("PR", c), False, True)])
+        tt(K("SVL", c), K("SV", c), K("VK", c), A.mult, ["SV" + n, "VK" + n], ["SVL" + n])
+        if t < LEVELS - 1:
+            ts(X("O1", c)[:], bb[:, 128:256], 0.0, A.is_equal, ["BB" + n], ["O1" + n])
+        tt(K("TP", c), K("SV", c), Lb[:, 256:384], A.mult, ["SV" + n], ["TP" + n], LB)
+        scan(K("VM", c), T.RM[:, 0:128], K("SVL", c), 0.0, A.mult, A.max, ["RM", "SVL" + n], ["VM" + n])
+        tt(TTb[:, :, 1, :], K("TP", c), Lb[:, 384:512], A.add, ["TP" + n], ["TTb" + n], LB)
+        tt(X("VT", c)[:], K("VM", c, 15, 128, 16), X("U3", c)[:], A.add, ["VM" + n, "U3" + n], ["VT" + n])
+        tt(TTb[:, :, 2, :], TTb[:, :, 1, :], TTb[:, :, 1, :], A.mult, ["TTb" + n], ["TTc" + n])
+        op("P", ["VT" + n, "LS"], [], LB, lambda: [
+            p.matmul(Lb[:, 128 + 8 * b:136 + 8 * b], T.LS[:, b], X("VT", c)[:], True, True) for b in range(8)])
+
+    def lists(c):
+        n = str(c)
+        Lb, LB = X("L", c), ["L" + n]
+        tt(X("LM", c)[:], T.DG[:], Lb[:, 128:192], A.mult, ["DG"], ["LM" + n], LB)
+        scan(X("LV", c)[:], T.RM8[:], X("LM", c)[:], 0.0, A.mult, A.add, ["RM8", "LM" + n], ["LV" + n])
+        copy(K("VI", c), X("LV", c)[:, 7::8], ["LV" + n], ["VI" + n])
+        ts(K("R", c, 0, 8), K("VI", c), 15, A.bitwise_and, ["VI" + n], ["Ra" + n])
+        ts(K("R", c, 8, 16), K("VI", c), 8, A.arith_shift_right, ["VI" + n], ["Rb" + n])
+        ts(K("R", c, 16, 24), K("VI", c), 4, A.arith_shift_right, ["VI" + n], ["Rc" + n], (), 15, A.bitwise_and)
+        rr = ["Ra" + n, "Rb" + n, "Rc" + n]
+        tt(K("R", c), K("R", c), T.MUL[:], A.mult, rr + ["MULa", "MULb", "MULc"], rr)
+        tt(K("R", c), K("R", c), X("AD", c)[:], A.add, rr + ["AD%d%s" % (c, j) for j in "abc"], rr)
+        copy(X("LST", c)[:], K("R", c), rr, ["LST" + n])
+
+    def maximum(c, x):
+        n = str(c)
+        scan(X(x + "S", c)[:], X(x + "G", c)[:], X("DS", c)[:], -1024.0, A.max, A.add,
+             [x + "G" + n] + ["DS%d_%d" % (c, m) for m in range(4)], [x + "S" + n])
+
+    def leave(t, c):
+        n = str(c)
+        xs, ys = X("XS", c)[:, 15::16], X("YS", c)[:, 15::16]
+        if t == LEVELS - 1:
+            ts(T.OS[:, :, c, :], ys, 1024.0, A.add, ["YS" + n], ["OS" + n])
+            ts(T.OZ[:, :, c, :], xs, 1024.0, A.add, ["XS" + n], ["OZ" + n])
+            return
+        key = "%d%d" % (t, c)
+        sz, rz = T["SZ" + key], T["RZ" + key]
+        ts(sz[:, :, 0:16], ys, 1024.0, A.add, ["YS" + n], ["SZa" + key])
+        ts(sz[:, :, 16:32], xs, 1024.0, A.add, ["XS" + n], ["SZb" + key])
+        sync("G", ["SZa" + key, "SZb" + key], [], [])
+        for call in calls_of(core, cores, topo):
+            g.remote_dma_fused([RemoteDMATransfer(
+                src=sz[:, cores.index(d), :], dst=rz[:, rank, :],
+                dst_ids=[DstId(rid=topo.addr(d, core)[0], pnc=topo.addr(d, core)[1])],
+                dma_engine_mask=sum(1 << e for e in en), remote_sem=T.sem["arr" + key]) for d, en in call],
+                local_sem=T.sem["snt" + key])
+        copy(rz[:, rank, :], sz[:, rank, :], ["SZa" + key, "SZb" + key], ["RZ" + key + "o"])
+        total = sum(len(en) for o in cores if o != core for call in calls_of(o, cores, topo) for d, en in call if d == core)
+        wr["RZ" + key] = ("arr" + key, total, {})
+
+    def order(c):
+        n = str(c)
+        TTb, TLb, FRb = X("TT", c), X("TL", c), X("FR", c)
+        bk = [(X("E", c), "E" + n), (X("Q", c), "Q" + n)]
+        op("P", ["TTa" + n, "TTb" + n, "TTc" + n, "ID3"], [], ["E" + n], lambda: [
+            p.matmul(bk[0][0][0:96, j], TTb[:, :, :, j::4], T.ID3[:], True, True) for j in range(4)])
+        op("S", [], ["TL" + n], ["E" + n], lambda: s.activation(TLb[0:96], bk[0][0][0:96], AF.Copy))
+        for j in range(4):
+            b, key = bk[(j + 1) & 1]
+            op("P", ["TL" + n, "FQ"], [], [key], lambda: [
+                p.matmul(b[:, i], T.FQ[0:96, i], TLb[0:96, j], True, True) for i in range(4)])
+            op("S", ["q6"], ["FR%d_%d" % (c, j)], [key],
+               lambda: s.activation(FRb[:, j], b[:], AF.Relu, bias=T.QC[:, 6:7]))
+        for j in range(4):
+            op("P", ["FR%d_%d" % (c, j), "ID"], [], ["Q" + n], lambda: [
+                p.matmul(bk[1][0][:, 0], T.ID[:], FRb[:, j, i], j == 0 and i == 0, j == 3 and i == 3) for i in range(4)])
+
+    def cwrite(c):
+        n = str(c)
+        copy(X("FC", c)[:], X("Q", c)[:, 0], [], ["FC" + n], ["Q" + n])
+        op("V", ["FC" + n, "LST" + n], ["CW"], [], lambda: v.tensor_copy(
+            T.CW[:, 0:1024].indirect(X("LST", c)[:, 8:16]), X("FC", c)[:]))
+
+    def xnew(c):
+        n = str(c)
+        ts(X("NZ", c)[:], X("XS", c)[:, 15::16], 1024.0, A.add, ["XS" + n], ["NZ" + n])
+        op("V", ["XG" + n, "LST" + n, "NZ" + n], ["XQ" + n], [], lambda: v.tensor_tensor(
+            X("XQ", c)[:], X("XG", c)[:, 0:2048].indirect(X("LST", c)[:, 16:24]), X("NZ", c)[:], A.add))
+        ts(X("XR", c)[:], X("XQ", c)[:], 1, A.arith_shift_right, ["XQ" + n], ["XR" + n])
+
+    def xwrite(c):
+        n = str(c)
+        op("V", ["XR" + n, "LST" + n], ["XW"], [], lambda: v.tensor_copy(
+            T.XW[:, 0:4096].indirect(X("LST", c)[:, 0:8]), X("XR", c)[:]))
+
+    def weights(a, b):
+        iota(T.DI[:, a:b], [[1, b - a], [0, 128]], a + 1, 0, ["DI%d" % a])
+        sel(T.DI[:, a:b], T.DI[:, a:b], [[0, b - a], [-1, 128]], A.is_equal, 0.0, 0, 1, ["DI%d" % a], ["DI%d" % a])
+
+    for t in range(LEVELS):
+        if t == 0:
+            seats(t, 0)
+            seats(t, 1)
+            ts(T.CW[:], T.CM[:], 1023, A.bitwise_and, ["CM"], ["CW"])
+        else:
+            seats(t, 0)
+        cgather("S", 0, 0, 64)
+        cgather("V", 0, 64, 128)
+        zrow(t, 0)
+        if t > 0:
+            seats(t, 1)
+        cgather("S", 1, 0, 64)
+        cgather("S", 1, 64, 128)
+        zrow(t, 1)
+        if t == 0:
+            ts(T.MW[:], T.CM[:], 10, A.arith_shift_right, ["CM"], ["MW"])
+        members(t, 0)
+        hashes(t, 0)
+        members(t, 1)
+        hashes(t, 1)
+        if t == 0:
+            late_constants()
+        xgather("S", 0)
+        xgather("S", 1)
+        survivors(t, 0)
+        spread(0)
+        mgather("S", 0)
+        places(t, 0)
+        survivors(t, 1)
+        spread(1)
+        mgather("S", 1)
+        places(t, 1)
+        maximum(0, "X")
+        maximum(0, "Y")
+        leave(t, 0)
+        maximum(1, "X")
+        order(0)
+        order(1)
+        lists(0)
+        maximum(1, "Y")
+        leave(t, 1)
+        if t < LEVELS - 1:
+            weights(32 * t, 32 * t + 16)
+            weights(32 * t + 16, 32 * t + 32)
+        lists(1)
+        xnew(0)
+        xnew(1)
+        xwrite(0)
+        xwrite(1)
+        cwrite(0)
+        cwrite(1)
+    dma("Y", "os", T.ys[:], T.OS[:], ["OS0", "OS1"], [])
+    dma("Y", "oz", T.yz[:], T.OZ[:], ["OZ0", "OZ1"], [])
+    dis = ["DI0", "DI16", "DI32", "DI48"]
+    op("P", ["XW"] + dis, [], ["L0"], lambda: [
+        p.matmul(T.L0[:, 0:64], T.DI[:, m], T.XW[:, 64 * m:64 * m + 64], m == 0, m == 63) for m in range(64)])
+    copy(T.CF[:], T.CW[:], ["CW"], ["CF"])
+    op("P", ["CF"] + dis, [], ["L1"], lambda: [
+        p.matmul(T.L1[:, 0:64], T.DI[:, m], T.CF[:, 64 * m:64 * m + 64], m == 0, m == 15) for m in range(16)])
+    copy(T.OX[:], T.L0[:, 0:64], [], ["OX"], ["L0"])
+    dma("Y", "ox", T.yx[:], T.OX[:], ["OX"], [])
+    copy(T.OC[:], T.L1[:, 0:64], [], ["OC"], ["L1"])
+    dma("Y", "oc", T.yc[:], T.OC[:], ["OC"], [])
+    for sem in sorted(cnt):
+        g.wait_ge(T.sem[sem], cnt[sem])
+    for t in range(LEVELS - 1):
+        for c in (0, 1):
+            g.wait_ge(T.sem["snt%d%d" % (t, c)], sum(len(en) for call in calls_of(core, cores, topo) for d, en in call))

@@ -8,7 +8,7 @@ LEVELS = 3
 _B, _H, _F, _I, _U = "bfloat16", "float16", "float32", "int32", "uint16"
 PACK, _w = {}, {}
 for _b, _n, _c in [("B7", x, 128) for x in ("VK", "SV", "AL", "PR", "TP", "SVL", "VM")] + [
-        ("IS", "UI", 16), ("IS", "KI", 32), ("IS", "KJ", 24), ("IS", "BN", 16), ("IS", "VI", 8), ("IS", "R", 24)]:
+        ("IS", "UI", 16), ("IS", "KI", 32), ("IS", "KJ", 24), ("IS", "BN", 16)]:
     PACK[_n] = (_b, _w.get(_b, 0), _c)
     _w[_b] = _w.get(_b, 0) + _c
 KP = {_n: 128 * _i for _i, _n in enumerate(("KM7", "KM2", "KC16", "NI", "I2"))}
@@ -18,13 +18,17 @@ SCRATCH = {
     "CF": ("sbuf", [128, 1024], _H),
     "ON2": ("sbuf", [128, 128], _B), "ON3": ("sbuf", [128, 8, 8, 16], _B), "ID": ("sbuf", [128, 128], _B),
     "ID3": ("sbuf", [128, 8, 16], _B), "BO": ("sbuf", [128, 8, 16], _B), "WB": ("sbuf", [128, 8], _B),
-    "LS": ("sbuf", [128, 8, 8, 16], _B), "DG": ("sbuf", [128, 64], _B), "FQ": ("sbuf", [128, 4, 8, 16], _B),
+    "LS": ("sbuf", [128, 8, 8, 16], _B), "DG": ("sbuf", [128, 128], _B), "FQ": ("sbuf", [128, 4, 8, 16], _B),
     "BK": ("sbuf", [128, 16, 8, 16], _B), "I613": ("sbuf", [128, 128], _H), "KP": ("sbuf", [128, 640], _B),
-    "RM": ("sbuf", [128, 512], _B), "RM8": ("sbuf", [128, 64], _B), "KCC": ("sbuf", [128, 32], _B),
-    "MUL": ("sbuf", [128, 24], _I), "AD0": ("sbuf", [128, 24], _I), "AD1": ("sbuf", [128, 24], _I),
-    "BS0": ("sbuf", [128, 24], _I), "BS1": ("sbuf", [128, 24], _I), "QI": ("sbuf", [128, 16], _I),
-    "QJ": ("sbuf", [128, 16], _I), "QC": ("sbuf", [128, 16], _F), "RA": ("sbuf", [128, 16], _F), "RB": ("sbuf", [128, 16], _F),
-    "DI": ("sbuf", [128, 64, 128], _B),
+    "RM": ("sbuf", [128, 512], _B), "RM8": ("sbuf", [128, 128], _B), "KCC": ("sbuf", [128, 32], _B),
+    "MUL": ("sbuf", [128, 48], _I), "AD": ("sbuf", [128, 48], _I), "BS": ("sbuf", [128, 48], _I),
+    "QI": ("sbuf", [128, 16], _I), "QJ": ("sbuf", [128, 16], _I), "QC": ("sbuf", [128, 16], _F),
+    "RA": ("sbuf", [128, 16], _F), "RB": ("sbuf", [128, 16], _F), "DI": ("sbuf", [128, 64, 128], _B),
+    "CG": ("sbuf", [128, 4096], _H), "YG": ("sbuf", [128, 4096], _H), "XG": ("sbuf", [128, 4096], _B),
+    "XS": ("sbuf", [128, 4096], _H), "YS": ("sbuf", [128, 4096], _H), "DS": ("sbuf", [128, 4096], _B),
+    "LM": ("sbuf", [128, 128], _H), "LV": ("sbuf", [128, 128], _H), "VI": ("sbuf", [128, 16], _I),
+    "RL": ("sbuf", [128, 48], _I), "LST": ("sbuf", [128, 48], _U), "NZ": ("sbuf", [128, 256], _H),
+    "XQ": ("sbuf", [128, 256], _I), "XR": ("sbuf", [128, 256], _I), "FC": ("sbuf", [128, 256], _F),
     "OS": ("sbuf", [128, 8, 2, 16], _F), "OZ": ("sbuf", [128, 8, 2, 16], _B),
     "OX": ("sbuf", [128, 64], _F), "OC": ("sbuf", [128, 64], _F),
     "D0": ("psum", [128, 512], _F), "D1": ("psum", [128, 512], _F),
@@ -35,8 +39,7 @@ for _c in "01":
         "L" + _c: ("psum", [128, 512], _F),
         "B7" + _c: ("sbuf", [128, _w["B7"]], _B), "IS" + _c: ("sbuf", [128, _w["IS"]], _I),
         "ZC" + _c: ("sbuf", [128, 128], _H), "OFS" + _c: ("sbuf", [128, 128], _U), "OFM" + _c: ("sbuf", [128, 128], _U),
-        "OFX" + _c: ("sbuf", [128, 128], _U), "CG" + _c: ("sbuf", [128, 2048], _H), "YG" + _c: ("sbuf", [128, 2048], _H),
-        "XG" + _c: ("sbuf", [128, 2048], _B), "XS" + _c: ("sbuf", [128, 2048], _H), "YS" + _c: ("sbuf", [128, 2048], _H),
+        "OFX" + _c: ("sbuf", [128, 128], _U),
         "ES" + _c: ("sbuf", [128, 8, 16], _H), "EQ" + _c: ("sbuf", [128, 15, 8, 16], _B),
         "U1" + _c: ("sbuf", [128, 8, 16], _F), "U3" + _c: ("sbuf", [128, 8], _F),
         "WI" + _c: ("sbuf", [128, 8, 16], _I), "HI" + _c: ("sbuf", [128, 8, 16], _I), "H8" + _c: ("sbuf", [128, 8, 16], _I),
@@ -44,10 +47,7 @@ for _c in "01":
         "IN" + _c: ("sbuf", [128, 512], _B), "CT" + _c: ("sbuf", [128, 512], _B), "KB" + _c: ("sbuf", [128, 256], _B),
         "BB" + _c: ("sbuf", [128, 256], _B),
         "TT" + _c: ("sbuf", [128, 8, 3, 16], _H), "TL" + _c: ("sbuf", [128, 4, 8, 16], _H),
-        "FR" + _c: ("sbuf", [128, 4, 4, 8, 16], _H), "FC" + _c: ("sbuf", [128, 128], _F), "O1" + _c: ("sbuf", [128, 8, 16], _B),
-        "VT" + _c: ("sbuf", [128, 8], _H), "LM" + _c: ("sbuf", [128, 64], _H), "LV" + _c: ("sbuf", [128, 64], _H),
-        "LST" + _c: ("sbuf", [128, 24], _U), "NZ" + _c: ("sbuf", [128, 128], _H),
-        "XQ" + _c: ("sbuf", [128, 128], _I), "XR" + _c: ("sbuf", [128, 128], _I), "DS" + _c: ("sbuf", [128, 2048], _B),
+        "FR" + _c: ("sbuf", [128, 16, 8, 16], _H), "O1" + _c: ("sbuf", [128, 8, 16], _B), "VT" + _c: ("sbuf", [128, 8], _H),
         "SZ0" + _c: ("sbuf", [128, 8, 32], _H), "SZ1" + _c: ("sbuf", [128, 8, 32], _H),
         "RZ0" + _c: ("sbuf", [128, 8, 32], _H), "RZ1" + _c: ("sbuf", [128, 8, 32], _H),
     })
@@ -154,6 +154,9 @@ def rank_program(g, core, T, topo):
         buf, off, w = PACK[name]
         return T[buf + str(c)][:, off + a:off + (w if b is None else b):st]
 
+    def fan(name, c, a=0, st=1):
+        return T[name][:, 2048 * c + a:2048 * c + 2048:st]
+
     def C(name):
         return T.KP[:, KP[name]:KP[name] + 128]
 
@@ -172,17 +175,15 @@ def rank_program(g, core, T, topo):
     iota(C("KM7"), [[0, 8], [1, 16]], -7, 0, ["KM7"])
     iota(C("KM2"), [[0, 8], [-1, 16]], -2, 0, ["KM2"])
     sel(T.LS[:], T.ON3[:], [[-16, 8], [0, 8], [-1, 16]], A.is_equal, 0.0, 0, 1, ["ON3"], ["LS"])
-    sel(T.DG[:], T.ON2[:, 0:64], [[0, 8], [-16, 8]], A.is_ge, 0.0, 0, 1, ["ON2"], ["DG"])
-    sel(T.DG[:], T.DG[:], [[0, 8], [16, 8]], A.is_ge, 0.0, 15, -1, ["DG"], ["DG"])
-    for c in (0, 1):
-        bs = X("BS", c)
-        iota(bs[:, 0:8], [[32, 8]], 16 * c, 0, ["BS%da" % c], False)
-        iota(bs[:, 8:16], [[128, 8]], 64 * c, 0, ["BS%db" % c], False)
-        iota(bs[:, 16:24], [[256, 8]], 15, 0, ["BS%dc" % c], False)
     iota(T.FQ[:], [[0, 4], [0, 8], [2048, 16]], -16384, 0, ["FQ"])
     sel(T.FQ[:], T.FQ[:], [[-1, 4], [-12, 8], [0, 16]], A.is_equal, 0.0, -4, 1, ["FQ"], ["FQ"])
     sel(T.FQ[:], T.FQ[:], [[-1, 4], [-12, 8], [0, 16]], A.not_equal, 1.0, 0, 1, ["FQ"], ["FQ"])
     sel(T.FQ[:], T.FQ[:], [[-1, 4], [-12, 8], [0, 16]], A.not_equal, -1024.0, -8, 1, ["FQ"], ["FQ"])
+    sel(T.DG[:], T.ON2[:], [[0, 16], [-16, 8]], A.is_ge, 0.0, 0, 1, ["ON2"], ["DG"])
+    sel(T.DG[:], T.DG[:], [[0, 16], [16, 8]], A.is_ge, 0.0, 15, -1, ["DG"], ["DG"])
+    iota(T.BS[:, 0:16], [[16, 2], [32, 8]], 0, 0, ["BSa"], False)
+    iota(T.BS[:, 16:32], [[64, 2], [128, 8]], 0, 0, ["BSb"], False)
+    iota(T.BS[:, 32:48], [[2048, 2], [256, 8]], 15, 0, ["BSc"], False)
     ts(T.QJ[:], T.QI[:], 15, A.bitwise_and, ["QI"], ["QJ"])
     q = T.QC
     copy(q[:, 0:1], T.QJ[:, 0:1], ["QJ"], ["q0"])
@@ -206,17 +207,16 @@ def rank_program(g, core, T, topo):
     fill(T.KB1[:], 0.0, ["KB1"])
     fill(T.RM[:, ::16], 0.0, ["RM"])
     fill(T.RM8[:, ::8], 0.0, ["RM8"])
-    fill(T.MUL[:, 0:8], 256, ["MULa"])
-    fill(T.MUL[:, 8:16], 1, ["MULb"])
-    fill(T.MUL[:, 16:24], -1, ["MULc"])
+    fill(T.MUL[:, 0:16], 256, ["MULa"])
+    fill(T.MUL[:, 16:32], 1, ["MULb"])
+    fill(T.MUL[:, 32:48], -1, ["MULc"])
     for k in range(16):
         ts(T.BK[:, k], T.BO[:], T.RA[:, k:k + 1], A.mult, ["BO", "RA"], ["BK%d" % k])
 
     def late_constants():
-        for c in (0, 1):
-            for j, n in ((0, 0), (1, 2), (2, 3)):
-                ts(X("AD", c)[:, 8 * j:8 * j + 8], X("BS", c)[:, 8 * j:8 * j + 8], q[:, n:n + 1], A.add,
-                   ["BS%d%s" % (c, "abc"[j]), "q%d" % n], ["AD%d%s" % (c, "abc"[j])])
+        for j, n in ((0, 0), (1, 2), (2, 3)):
+            ts(T.AD[:, 16 * j:16 * j + 16], T.BS[:, 16 * j:16 * j + 16], q[:, n:n + 1], A.add,
+               ["BS" + "abc"[j], "q%d" % n], ["AD" + "abc"[j]])
 
     def gather(e, out, win, off, R, W):
         if e == "V":
@@ -244,15 +244,24 @@ def rank_program(g, core, T, topo):
             p.matmul(Eb[:, 1], X("ZC", c)[:], T.BO[:], True, True),
             p.matmul(Eb[:, 2, :, 0], X("ZC", c)[:], T.BO[:, :, 0], True, True)])
 
+    def part(name, c, a, b):
+        return T[name][:, 2048 * c + 16 * a:2048 * c + 16 * b]
+
     def cgather(e, c, a, b):
-        n = str(c)
-        gather(e, X("CG", c)[:, 16 * a:16 * b], T.CW[:, 0:1024], X("OFS", c)[:, a:b], ["CW", "OFS" + n],
+        gather(e, part("CG", c, a, b), T.CW[:, 0:1024], X("OFS", c)[:, a:b], ["CW", "OFS%d" % c],
                ["CG%d%s" % (c, "b" if a else "a")])
+
+    def mgather(e, c, a, b):
+        gather(e, part("YG", c, a, b), T.MW[:, 0:1024], X("OFM", c)[:, a:b], ["MW", "OFM%d" % c],
+               ["YG%d%s" % (c, "b" if a else "a")])
+
+    def xgather(e, c):
+        gather(e, fan("XG", c), T.XW[:, 0:4096], X("OFX", c)[:, 0:128], ["XW", "OFX%d" % c], ["XG%d" % c])
 
     def members(t, c):
         n = str(c)
         op("P", ["CG" + n + "a", "CG" + n + "b", "ID"], [], ["E" + n], lambda: [
-            p.matmul(X("E", c)[:, 0, :, k], X("CG", c)[:, k::16], T.ID[:, (k + t) & 15::16], True, True) for k in range(16)])
+            p.matmul(X("E", c)[:, 0, :, k], fan("CG", c, k, 16), T.ID[:, (k + t) & 15::16], True, True) for k in range(16)])
 
     def hashes(t, c):
         n = str(c)
@@ -299,20 +308,15 @@ def rank_program(g, core, T, topo):
         ts(X("OFX", c)[:], Lb[:, 0:128], 2048.0, A.add, [], ["OFX" + n], ["L" + n])
         tt(K("VK", c), X("H8", c)[:], C("KC16"), A.add, ["H8" + n, "KC16"], ["VK" + n])
 
-    def mgather(e, c):
+    def bins(c):
         n = str(c)
-        gather(e, X("YG", c)[:], T.MW[:, 0:1024], X("OFM", c)[:, 0:128], ["MW", "OFM" + n], ["YG" + n])
-
-    def xgather(e, c):
-        n = str(c)
-        gather(e, X("XG", c)[:], T.XW[:, 0:4096], X("OFX", c)[:, 0:128], ["XW", "OFX" + n], ["XG" + n])
+        op("P", ["XG" + n, "WB"], [], ["L" + n], lambda: [
+            p.matmul(X("L", c)[:, 128 + k:256:16], fan("XG", c, k, 16), T.WB[:], True, True) for k in range(16)])
 
     def survivors(t, c):
         n = str(c)
         Lb, LB = X("L", c), ["L" + n]
-        xg, bi, ind = X("XG", c), X("BI", c), X("IN", c)
-        op("P", ["XG" + n, "WB"], [], LB, lambda: [
-            p.matmul(Lb[:, 128 + k:256:16], xg[:, k::16], T.WB[:], True, True) for k in range(16)])
+        bi, ind = X("BI", c), X("IN", c)
         copy(bi[:], Lb[:, 128:256], [], ["BI" + n], LB)
         ts(bi[:], bi[:], 3, A.bitwise_and, ["BI" + n], ["BI" + n])
         ink = ["IN%d_%d" % (c, b) for b in range(4)]
@@ -332,20 +336,19 @@ def rank_program(g, core, T, topo):
         scan(K("PR", c), T.RM[:, 0:128], K("SV", c), 0.0, A.mult, A.add, ["RM", "SV" + n], ["PR" + n])
         ts(K("AL", c), Lb[:, 0:128], -2.0, A.add, [], ["AL" + n], LB)
 
-    def spread(c):
+    def spread(c, ms):
         n = str(c)
         bks = ["BK%d" % k for k in range(16)]
-        for m in range(4):
+        for m in ms:
             D, db = T["D%d" % (m & 1)], "D%d" % (m & 1)
             op("P", ["AL" + n] + bks, [], [db], lambda: [
                 p.matmul(D[:, 128 * j:128 * j + 128], T.BK[:, 4 * m + j], K("AL", c), True, True) for j in range(4)])
             op("S", [], ["DS%d_%d" % (c, m)], [db], lambda: [
-                s.activation(X("DS", c)[:, 4 * m + j::16], D[:, 128 * j:128 * j + 128], AF.Copy) for j in range(4)])
+                s.activation(fan("DS", c, 4 * m + j, 16), D[:, 128 * j:128 * j + 128], AF.Copy) for j in range(4)])
 
-    def places(t, c):
+    def ranks(c):
         n = str(c)
-        Lb, LB = X("L", c), ["L" + n]
-        bb, TTb = X("BB", c), X("TT", c)
+        Lb, LB, bb = X("L", c), ["L" + n], X("BB", c)
         op("P", ["PR" + n, "BB" + n, "ID", "NI", "I2", "KM7", "KM2"], [], LB, lambda: [
             p.matmul(Lb[:, 384:512], T.ID[:], bb[:, 128:256], True, False),
             p.matmul(Lb[:, 384:512], T.ID[:], C("KM7"), False, False),
@@ -353,6 +356,11 @@ def rank_program(g, core, T, topo):
             p.matmul(Lb[:, 256:384], C("NI"), bb[:, 128:256], True, False),
             p.matmul(Lb[:, 256:384], T.ID[:], C("KM2"), False, False),
             p.matmul(Lb[:, 256:384], C("I2"), K("PR", c), False, True)])
+
+    def places(t, c):
+        n = str(c)
+        Lb, LB = X("L", c), ["L" + n]
+        bb, TTb = X("BB", c), X("TT", c)
         tt(K("SVL", c), K("SV", c), K("VK", c), A.mult, ["SV" + n, "VK" + n], ["SVL" + n])
         if t < LEVELS - 1:
             ts(X("O1", c)[:], bb[:, 128:256], 0.0, A.is_equal, ["BB" + n], ["O1" + n])
@@ -361,31 +369,35 @@ def rank_program(g, core, T, topo):
         tt(TTb[:, :, 1, :], K("TP", c), Lb[:, 384:512], A.add, ["TP" + n], ["TTb" + n], LB)
         tt(X("VT", c)[:], K("VM", c, 15, 128, 16), X("U3", c)[:], A.add, ["VM" + n, "U3" + n], ["VT" + n])
         tt(TTb[:, :, 2, :], TTb[:, :, 1, :], TTb[:, :, 1, :], A.mult, ["TTb" + n], ["TTc" + n])
-        op("P", ["VT" + n, "LS"], [], LB, lambda: [
-            p.matmul(Lb[:, 128 + 8 * b:136 + 8 * b], T.LS[:, b], X("VT", c)[:], True, True) for b in range(8)])
 
-    def lists(c):
+    def turn(c):
         n = str(c)
-        Lb, LB = X("L", c), ["L" + n]
-        tt(X("LM", c)[:], T.DG[:], Lb[:, 128:192], A.mult, ["DG"], ["LM" + n], LB)
-        scan(X("LV", c)[:], T.RM8[:], X("LM", c)[:], 0.0, A.mult, A.add, ["RM8", "LM" + n], ["LV" + n])
-        copy(K("VI", c), X("LV", c)[:, 7::8], ["LV" + n], ["VI" + n])
-        ts(K("R", c, 0, 8), K("VI", c), 15, A.bitwise_and, ["VI" + n], ["Ra" + n])
-        ts(K("R", c, 8, 16), K("VI", c), 8, A.arith_shift_right, ["VI" + n], ["Rb" + n])
-        ts(K("R", c, 16, 24), K("VI", c), 4, A.arith_shift_right, ["VI" + n], ["Rc" + n], (), 15, A.bitwise_and)
-        rr = ["Ra" + n, "Rb" + n, "Rc" + n]
-        tt(K("R", c), K("R", c), T.MUL[:], A.mult, rr + ["MULa", "MULb", "MULc"], rr)
-        tt(K("R", c), K("R", c), X("AD", c)[:], A.add, rr + ["AD%d%s" % (c, j) for j in "abc"], rr)
-        copy(X("LST", c)[:], K("R", c), rr, ["LST" + n])
+        o = 128 + 64 * c
+        op("P", ["VT" + n, "LS"], [], ["L0"], lambda: [
+            p.matmul(T.L0[:, o + 8 * b:o + 8 * b + 8], T.LS[:, b], X("VT", c)[:], True, True) for b in range(8)])
+
+    def lists():
+        r = T.RL
+        tt(T.LM[:], T.DG[:], T.L0[:, 128:256], A.mult, ["DG"], ["LM"], ["L0"])
+        scan(T.LV[:], T.RM8[:], T.LM[:], 0.0, A.mult, A.add, ["RM8", "LM"], ["LV"])
+        copy(T.VI[:], T.LV[:, 7::8], ["LV"], ["VI"])
+        ts(r[:, 0:16], T.VI[:], 15, A.bitwise_and, ["VI"], ["Ra"])
+        ts(r[:, 16:32], T.VI[:], 8, A.arith_shift_right, ["VI"], ["Rb"])
+        ts(r[:, 32:48], T.VI[:], 4, A.arith_shift_right, ["VI"], ["Rc"], (), 15, A.bitwise_and)
+        rr = ["Ra", "Rb", "Rc"]
+        tt(r[:], r[:], T.MUL[:], A.mult, rr + ["MULa", "MULb", "MULc"], rr)
+        tt(r[:], r[:], T.AD[:], A.add, rr + ["ADa", "ADb", "ADc"], rr)
+        copy(T.LST[:], r[:], rr, ["LST"])
 
     def maximum(c, x):
         n = str(c)
-        scan(X(x + "S", c)[:], X(x + "G", c)[:], X("DS", c)[:], -1024.0, A.max, A.add,
-             [x + "G" + n] + ["DS%d_%d" % (c, m) for m in range(4)], [x + "S" + n])
+        src = ["XG" + n] if x == "X" else ["YG" + n + "a", "YG" + n + "b"]
+        scan(fan(x + "S", c), fan(x + "G", c), fan("DS", c), -1024.0, A.max, A.add,
+             src + ["DS%d_%d" % (c, m) for m in range(4)], [x + "S" + n])
 
     def leave(t, c):
         n = str(c)
-        xs, ys = X("XS", c)[:, 15::16], X("YS", c)[:, 15::16]
+        xs, ys = fan("XS", c, 15, 16), fan("YS", c, 15, 16)
         if t == LEVELS - 1:
             ts(T.OS[:, :, c, :], ys, 1024.0, A.add, ["YS" + n], ["OS" + n])
             ts(T.OZ[:, :, c, :], xs, 1024.0, A.add, ["XS" + n], ["OZ" + n])
@@ -405,52 +417,47 @@ def rank_program(g, core, T, topo):
         total = sum(len(en) for o in cores if o != core for call in calls_of(o, cores, topo) for d, en in call if d == core)
         wr["RZ" + key] = ("arr" + key, total, {})
 
-    def order(c):
+    def features(c):
         n = str(c)
-        TTb, TLb, FRb = X("TT", c), X("TL", c), X("FR", c)
-        bk = [(X("E", c), "E" + n), (X("Q", c), "Q" + n)]
         op("P", ["TTa" + n, "TTb" + n, "TTc" + n, "ID3"], [], ["E" + n], lambda: [
-            p.matmul(bk[0][0][0:96, j], TTb[:, :, :, j::4], T.ID3[:], True, True) for j in range(4)])
-        op("S", [], ["TL" + n], ["E" + n], lambda: s.activation(TLb[0:96], bk[0][0][0:96], AF.Copy))
-        for j in range(4):
-            b, key = bk[(j + 1) & 1]
-            op("P", ["TL" + n, "FQ"], [], [key], lambda: [
-                p.matmul(b[:, i], T.FQ[0:96, i], TLb[0:96, j], True, True) for i in range(4)])
-            op("S", ["q6"], ["FR%d_%d" % (c, j)], [key],
-               lambda: s.activation(FRb[:, j], b[:], AF.Relu, bias=T.QC[:, 6:7]))
-        for j in range(4):
-            op("P", ["FR%d_%d" % (c, j), "ID"], [], ["Q" + n], lambda: [
-                p.matmul(bk[1][0][:, 0], T.ID[:], FRb[:, j, i], j == 0 and i == 0, j == 3 and i == 3) for i in range(4)])
+            p.matmul(X("E", c)[0:96, j], X("TT", c)[:, :, :, j::4], T.ID3[:], True, True) for j in range(4)])
+        op("S", [], ["TL" + n], ["E" + n], lambda: s.activation(X("TL", c)[0:96], X("E", c)[0:96], AF.Copy))
 
-    def cwrite(c):
+    def pick(c, j):
         n = str(c)
-        copy(X("FC", c)[:], X("Q", c)[:, 0], [], ["FC" + n], ["Q" + n])
-        op("V", ["FC" + n, "LST" + n], ["CW"], [], lambda: v.tensor_copy(
-            T.CW[:, 0:1024].indirect(X("LST", c)[:, 8:16]), X("FC", c)[:]))
+        b, key = (X("E", c), "E" + n) if j & 1 else (X("Q", c), "Q" + n)
+        op("P", ["TL" + n, "FQ"], [], [key], lambda: [
+            p.matmul(b[:, i], T.FQ[0:96, i], X("TL", c)[0:96, j], True, True) for i in range(4)])
+        op("S", ["q6"], ["FR%d_%d" % (c, j)], [key],
+           lambda: s.activation(X("FR", c)[:, 4 * j:4 * j + 4], b[:], AF.Relu, bias=T.QC[:, 6:7]))
 
-    def xnew(c):
-        n = str(c)
-        ts(X("NZ", c)[:], X("XS", c)[:, 15::16], 1024.0, A.add, ["XS" + n], ["NZ" + n])
-        op("V", ["XG" + n, "LST" + n, "NZ" + n], ["XQ" + n], [], lambda: v.tensor_tensor(
-            X("XQ", c)[:], X("XG", c)[:, 0:2048].indirect(X("LST", c)[:, 16:24]), X("NZ", c)[:], A.add))
-        ts(X("XR", c)[:], X("XQ", c)[:], 1, A.arith_shift_right, ["XQ" + n], ["XR" + n])
+    def total(c, j):
+        op("P", ["FR%d_%d" % (c, j), "ID"], [], ["E0"], lambda: [
+            p.matmul(T.E0[:, c], T.ID[:], X("FR", c)[:, i], i == 0, i == 15) for i in range(4 * j, 4 * j + 4)])
 
-    def xwrite(c):
-        n = str(c)
-        op("V", ["XR" + n, "LST" + n], ["XW"], [], lambda: v.tensor_copy(
-            T.XW[:, 0:4096].indirect(X("LST", c)[:, 0:8]), X("XR", c)[:]))
+    def cwrite():
+        copy(T.FC[:], T.E0[:, 0:2], [], ["FC"], ["E0"])
+        op("V", ["FC", "LST"], ["CW"], [], lambda: v.tensor_copy(T.CW[:, 0:1024].indirect(T.LST[:, 16:32]), T.FC[:]))
+
+    def xnew():
+        ts(T.NZ[:], T.XS[:, 15::16], 1024.0, A.add, ["XS0", "XS1"], ["NZ"])
+        op("V", ["XG0", "XG1", "LST", "NZ"], ["XQ"], [], lambda: v.tensor_tensor(
+            T.XQ[:], T.XG[:, 0:4096].indirect(T.LST[:, 32:48]), T.NZ[:], A.add))
+        ts(T.XR[:], T.XQ[:], 1, A.arith_shift_right, ["XQ"], ["XR"])
+
+    def xwrite():
+        op("V", ["XR", "LST"], ["XW"], [], lambda: v.tensor_copy(T.XW[:, 0:4096].indirect(T.LST[:, 0:16]), T.XR[:]))
 
     def weights(a, b):
         iota(T.DI[:, a:b], [[1, b - a], [0, 128]], a + 1, 0, ["DI%d" % a])
         sel(T.DI[:, a:b], T.DI[:, a:b], [[0, b - a], [-1, 128]], A.is_equal, 0.0, 0, 1, ["DI%d" % a], ["DI%d" % a])
 
     for t in range(LEVELS):
+        last = t == LEVELS - 1
+        seats(t, 0)
         if t == 0:
-            seats(t, 0)
             seats(t, 1)
             ts(T.CW[:], T.CM[:], 1023, A.bitwise_and, ["CM"], ["CW"])
-        else:
-            seats(t, 0)
         cgather("S", 0, 0, 64)
         cgather("V", 0, 64, 128)
         zrow(t, 0)
@@ -461,41 +468,63 @@ def rank_program(g, core, T, topo):
         zrow(t, 1)
         if t == 0:
             ts(T.MW[:], T.CM[:], 10, A.arith_shift_right, ["CM"], ["MW"])
+        else:
+            xnew()
         members(t, 0)
         hashes(t, 0)
-        members(t, 1)
-        hashes(t, 1)
+        mgather("S", 0, 0, 64)
         if t == 0:
             late_constants()
+        else:
+            xwrite()
+        members(t, 1)
         xgather("S", 0)
+        hashes(t, 1)
         xgather("S", 1)
+        mgather("S", 1, 0, 64)
+        bins(0)
+        bins(1)
         survivors(t, 0)
-        spread(0)
-        mgather("S", 0)
+        ranks(0)
+        spread(0, (0, 1, 2, 3))
         places(t, 0)
+        features(0)
+        for j in range(4):
+            pick(0, j)
+        mgather("V", 0, 64, 128)
+        mgather("S", 1, 64, 128)
         survivors(t, 1)
-        spread(1)
-        mgather("S", 1)
+        ranks(1)
+        spread(1, (0, 1))
         places(t, 1)
+        features(1)
+        turn(0)
+        turn(1)
+        spread(1, (2, 3))
+        for j in range(4):
+            total(0, j)
+        pick(1, 0)
+        pick(1, 1)
+        total(1, 0)
+        pick(1, 2)
+        total(1, 1)
+        pick(1, 3)
+        total(1, 2)
+        total(1, 3)
         maximum(0, "X")
         maximum(0, "Y")
         leave(t, 0)
         maximum(1, "X")
-        order(0)
-        order(1)
-        lists(0)
         maximum(1, "Y")
         leave(t, 1)
-        if t < LEVELS - 1:
+        if not last:
             weights(32 * t, 32 * t + 16)
             weights(32 * t + 16, 32 * t + 32)
-        lists(1)
-        xnew(0)
-        xnew(1)
-        xwrite(0)
-        xwrite(1)
-        cwrite(0)
-        cwrite(1)
+        lists()
+        if last:
+            xnew()
+            xwrite()
+        cwrite()
     dma("Y", "os", T.ys[:], T.OS[:], ["OS0", "OS1"], [])
     dma("Y", "oz", T.yz[:], T.OZ[:], ["OZ0", "OZ1"], [])
     dis = ["DI0", "DI16", "DI32", "DI48"]

from concourse.bass import DstId, RemoteDMATransfer
from concourse.mybir import dt, AluOpType, AxisListType, ActivationFunctionType

A = AluOpType
AF = ActivationFunctionType
LEVELS = 3

_B, _H, _F, _I, _U = "bfloat16", "float16", "float32", "int32", "uint16"
PACK, _w = {}, {}
for _b, _n, _c in [("B7", x, 128) for x in ("VK", "SV", "AL", "PR", "TP", "SVL", "VM")] + [
        ("IS", "UI", 16), ("IS", "KI", 32), ("IS", "KJ", 24), ("IS", "BN", 16)]:
    PACK[_n] = (_b, _w.get(_b, 0), _c)
    _w[_b] = _w.get(_b, 0) + _c
KP = {_n: 128 * _i for _i, _n in enumerate(("KM7", "KM2", "KC16", "NI", "I2"))}
SCRATCH = {
    "XW": ("sbuf", [128, 4096], _B), "CM": ("sbuf", [128, 1024], _I), "CW": ("sbuf", [128, 1024], _I),
    "MW": ("sbuf", [128, 1024], _I), "S3": ("sbuf", [128, 8, 2, 16], _I), "Z3": ("sbuf", [128, 8, 2, 16], _B),
    "CF": ("sbuf", [128, 1024], _H),
    "ON2": ("sbuf", [128, 128], _B), "ON3": ("sbuf", [128, 8, 8, 16], _B), "ID": ("sbuf", [128, 128], _B),
    "ID3": ("sbuf", [128, 8, 16], _B), "BO": ("sbuf", [128, 8, 16], _B), "WB": ("sbuf", [128, 8], _B),
    "LS": ("sbuf", [128, 8, 8, 16], _B), "DG": ("sbuf", [128, 128], _B), "FQ": ("sbuf", [128, 4, 8, 16], _B),
    "BK": ("sbuf", [128, 16, 8, 16], _B), "I613": ("sbuf", [128, 128], _H), "KP": ("sbuf", [128, 640], _B),
    "RM": ("sbuf", [128, 512], _B), "RM8": ("sbuf", [128, 128], _B), "KCC": ("sbuf", [128, 32], _B),
    "MUL": ("sbuf", [128, 48], _I), "AD": ("sbuf", [128, 48], _I), "BS": ("sbuf", [128, 48], _I),
    "QI": ("sbuf", [128, 16], _I), "QJ": ("sbuf", [128, 16], _I), "QC": ("sbuf", [128, 16], _F),
    "RA": ("sbuf", [128, 16], _F), "RB": ("sbuf", [128, 16], _F), "DI": ("sbuf", [128, 64, 128], _B),
    "CG": ("sbuf", [128, 4096], _H), "YG": ("sbuf", [128, 4096], _H), "XG": ("sbuf", [128, 4096], _B),
    "XS": ("sbuf", [128, 4096], _H), "YS": ("sbuf", [128, 4096], _H), "DS": ("sbuf", [128, 4096], _B),
    "LM": ("sbuf", [128, 128], _H), "LV": ("sbuf", [128, 128], _H), "VI": ("sbuf", [128, 16], _I),
    "RL": ("sbuf", [128, 48], _I), "LST": ("sbuf", [128, 48], _U), "NZ": ("sbuf", [128, 256], _H),
    "XQ": ("sbuf", [128, 256], _I), "XR": ("sbuf", [128, 256], _I), "FC": ("sbuf", [128, 256], _F),
    "OS": ("sbuf", [128, 8, 2, 16], _F), "OZ": ("sbuf", [128, 8, 2, 16], _B),
    "OX": ("sbuf", [128, 64], _F), "OC": ("sbuf", [128, 64], _F),
    "D0": ("psum", [128, 512], _F), "D1": ("psum", [128, 512], _F),
}
for _c in "01":
    SCRATCH.update({
        "E" + _c: ("psum", [128, 4, 8, 16], _F), "Q" + _c: ("psum", [128, 4, 8, 16], _F),
        "L" + _c: ("psum", [128, 512], _F),
        "B7" + _c: ("sbuf", [128, _w["B7"]], _B), "IS" + _c: ("sbuf", [128, _w["IS"]], _I),
        "ZC" + _c: ("sbuf", [128, 128], _H), "OFS" + _c: ("sbuf", [128, 128], _U), "OFM" + _c: ("sbuf", [128, 128], _U),
        "OFX" + _c: ("sbuf", [128, 128], _U),
        "ES" + _c: ("sbuf", [128, 8, 16], _H), "EQ" + _c: ("sbuf", [128, 15, 8, 16], _B),
        "U1" + _c: ("sbuf", [128, 8, 16], _F), "U3" + _c: ("sbuf", [128, 8], _F),
        "WI" + _c: ("sbuf", [128, 8, 16], _I), "HI" + _c: ("sbuf", [128, 8, 16], _I), "H8" + _c: ("sbuf", [128, 8, 16], _I),
        "HF" + _c: ("sbuf", [128, 8, 16], _H), "BI" + _c: ("sbuf", [128, 128], _I),
        "IN" + _c: ("sbuf", [128, 512], _B), "CT" + _c: ("sbuf", [128, 512], _B), "KB" + _c: ("sbuf", [128, 256], _B),
        "BB" + _c: ("sbuf", [128, 256], _B),
        "TT" + _c: ("sbuf", [128, 8, 3, 16], _H), "TL" + _c: ("sbuf", [128, 4, 8, 16], _H),
        "FR" + _c: ("sbuf", [128, 16, 8, 16], _H), "O1" + _c: ("sbuf", [128, 8, 16], _B), "VT" + _c: ("sbuf", [128, 8], _H),
        "SZ0" + _c: ("sbuf", [128, 8, 32], _H), "SZ1" + _c: ("sbuf", [128, 8, 32], _H),
        "RZ0" + _c: ("sbuf", [128, 8, 32], _H), "RZ1" + _c: ("sbuf", [128, 8, 32], _H),
    })
SEMAPHORES = ["V", "S", "P", "G", "ds", "dz", "dc", "dx", "os", "oz", "ox", "oc"] + [
    k + t + c for k in ("arr", "snt") for t in "01" for c in "01"]


def calls_of(src, cores, topo):
    here = [c for c in topo.cores_of(src) if c in cores and c != src]
    off = [c for c in cores if c != src and c not in here]
    off.sort(key=lambda c: (2 if topo.mates(src, c) else 1 if topo.same_plane(src, c) else 0, c))
    eng = topo.engines(src, off[0])
    half = len(off) - 2
    w = len(eng) // half
    first = [(d, eng[w * i:w * i + w]) for i, d in enumerate(off[:half])]
    w = len(eng) // 2
    second = [(d, eng[w * i:w * i + w]) for i, d in enumerate(off[half:])]
    for d in here:
        second.append((d, [e for e in topo.engines(src, d) if e not in eng]))
    return [first, second]


def rank_program(g, core, T, topo):
    rank = T.rank_of(core)
    if rank is None:
        return
    cores = list(T.cores)
    E = {"V": g.vector, "S": g.scalar, "P": g.tensor, "G": g, "Y": g.sync}
    cnt, known = {}, {e: {} for e in E}
    wr, rd, bank = {}, {}, {}

    def sync(e, R, W, B):
        need = {}
        toks = [wr[r] for r in list(R) + list(W) if r in wr]
        for w in W:
            toks += list(rd.get(w, {}).values())
        for b in B:
            toks += [t for f, t in bank.get(b, {}).items() if f != e]
        for t in toks:
            if t[0] not in need or need[t[0]][1] < t[1]:
                need[t[0]] = t
        for sem in sorted(need, key=lambda x: x == e):
            sm, val, clk = need[sem]
            if known[e].get(sm, 0) < val:
                E[e].wait_ge(T.sem[sm], val)
                for k2, v2 in clk.items():
                    known[e][k2] = max(known[e].get(k2, 0), v2)
                known[e][sm] = val

    def note(e, tok, R, W, B):
        for w in W:
            wr[w] = tok
            rd[w] = {}
        for r in R:
            rd.setdefault(r, {})[tok[0]] = tok
        for b in B:
            bank.setdefault(b, {})[e] = tok

    def op(e, R, W, B, f):
        sync(e, R, W, B)
        ins = f()
        for i in (ins if isinstance(ins, list) else [ins]):
            i.then_inc(T.sem[e], 1)
            cnt[e] = cnt.get(e, 0) + 1
        note(e, (e, cnt[e], dict(known[e])), R, W, B)

    def dma(e, sem, out, in_, R, W):
        sync(e, R, W, [])
        E[e].dma_start(out, in_).then_inc(T.sem[sem], 16)
        cnt[sem] = cnt.get(sem, 0) + 16
        note(e, (sem, cnt[sem], dict(known[e])), R, W, [])

    v, s, p = g.vector, g.scalar, g.tensor

    def copy(out, in_, R, W, B=()):
        op("V", R, W, B, lambda: v.tensor_copy(out, in_))

    def ts(out, in0, s1, op0, R, W, B=(), s2=None, op1=None):
        if op1 is None:
            op("V", R, W, B, lambda: v.tensor_scalar(out, in0, s1, None, op0))
        else:
            op("V", R, W, B, lambda: v.tensor_scalar(out, in0, s1, s2, op0, op1))

    def tt(out, a, b, o, R, W, B=()):
        op("V", R, W, B, lambda: v.tensor_tensor(out, a, b, o))

    def scan(out, a, b, ini, o0, o1, R, W, B=()):
        op("V", R, W, B, lambda: v.tensor_tensor_scan(out, a, b, ini, o0, o1))

    def fill(ap, x, W):
        op("V", [], W, [], lambda: v.memset(ap, x))

    def iota(out, pat, base, cm, W, small=True):
        op("G", [], W, [], lambda: g.iota(out, pat, base, cm, allow_small_or_imprecise_dtypes=True) if small
           else g.iota(out, pat, base, cm))

    def sel(out, in_, pat, cmp, fl, base, cm, R, W):
        op("G", R, W, [], lambda: g.affine_select(out, in_, pat, cmp, fl, base, cm))

    def X(name, c):
        return T[name + str(c)]

    def K(name, c, a=0, b=None, st=1):
        buf, off, w = PACK[name]
        return T[buf + str(c)][:, off + a:off + (w if b is None else b):st]

    def fan(name, c, a=0, st=1):
        return T[name][:, 2048 * c + a:2048 * c + 2048:st]

    def C(name):
        return T.KP[:, KP[name]:KP[name] + 128]

    dma("S", "dc", T.CM[:], T.cm[:], [], ["CM"])
    dma("Y", "ds", T.S3[:], T.s0[:], [], ["S3"])
    dma("Y", "dz", T.Z3[:], T.z0[:], [], ["Z3"])
    dma("Y", "dx", T.XW[:], T.x0[:], [], ["XW"])
    fill(T.ON2[:], 1.0, ["ON2"])
    fill(T.ON3[:], 1.0, ["ON3"])
    iota(T.QI[:], [[-1, 16]], 0, 1, ["QI"], False)
    sel(T.ID[:], T.ON2[:], [[-1, 128]], A.is_equal, 0.0, 0, 1, ["ON2"], ["ID"])
    sel(T.BO[:], T.ON3[:, 0], [[-16, 8], [0, 16]], A.is_ge, 0.0, 0, 1, ["ON3"], ["BO"])
    sel(T.BO[:], T.BO[:], [[16, 8], [0, 16]], A.is_ge, 0.0, 15, -1, ["BO"], ["BO"])
    iota(C("KC16"), [[0, 8], [-16, 16]], 240, 0, ["KC16"])
    iota(T.KCC[:], [[1, 4], [0, 8]], -4, 0, ["KCC"])
    iota(C("KM7"), [[0, 8], [1, 16]], -7, 0, ["KM7"])
    iota(C("KM2"), [[0, 8], [-1, 16]], -2, 0, ["KM2"])
    sel(T.LS[:], T.ON3[:], [[-16, 8], [0, 8], [-1, 16]], A.is_equal, 0.0, 0, 1, ["ON3"], ["LS"])
    iota(T.FQ[:], [[0, 4], [0, 8], [2048, 16]], -16384, 0, ["FQ"])
    sel(T.FQ[:], T.FQ[:], [[-1, 4], [-12, 8], [0, 16]], A.is_equal, 0.0, -4, 1, ["FQ"], ["FQ"])
    sel(T.FQ[:], T.FQ[:], [[-1, 4], [-12, 8], [0, 16]], A.not_equal, 1.0, 0, 1, ["FQ"], ["FQ"])
    sel(T.FQ[:], T.FQ[:], [[-1, 4], [-12, 8], [0, 16]], A.not_equal, -1024.0, -8, 1, ["FQ"], ["FQ"])
    sel(T.DG[:], T.ON2[:], [[0, 16], [-16, 8]], A.is_ge, 0.0, 0, 1, ["ON2"], ["DG"])
    sel(T.DG[:], T.DG[:], [[0, 16], [16, 8]], A.is_ge, 0.0, 15, -1, ["DG"], ["DG"])
    iota(T.BS[:, 0:16], [[16, 2], [32, 8]], 0, 0, ["BSa"], False)
    iota(T.BS[:, 16:32], [[64, 2], [128, 8]], 0, 0, ["BSb"], False)
    iota(T.BS[:, 32:48], [[2048, 2], [256, 8]], 15, 0, ["BSc"], False)
    ts(T.QJ[:], T.QI[:], 15, A.bitwise_and, ["QI"], ["QJ"])
    q = T.QC
    copy(q[:, 0:1], T.QJ[:, 0:1], ["QJ"], ["q0"])
    fill(T.RM[:], 1.0, ["RM"])
    ts(q[:, 1:2], q[:, 0:1], 2.0, A.mult, ["q0"], ["q1"], (), 1.0, A.add)
    ts(q[:, 2:3], q[:, 0:1], 4.0, A.mult, ["q0"], ["q2"])
    ts(q[:, 3:4], q[:, 0:1], 16.0, A.mult, ["q0"], ["q3"])
    ts(q[:, 4:5], q[:, 0:1], -8.0, A.add, ["q0"], ["q4"])
    ts(T.RA[:], T.QJ[:], 0, A.is_equal, ["QJ"], ["RA"], (), 1024.0, A.mult)
    ts(T.RB[:], T.QJ[:], 1, A.is_equal, ["QJ"], ["RB"], (), 1024.0, A.mult)
    tt(q[:, 5:6], q[:, 4:5], q[:, 4:5], A.mult, ["q4"], ["q5"])
    tt(T.RA[:, 0:15], T.RA[:, 0:15], T.RB[:, 0:15], A.subtract, ["RA", "RB"], ["RA"])
    ts(q[:, 6:7], q[:, 5:6], -1024.0, A.mult, ["q5"], ["q6"])
    copy(T.ID3[:], T.ID[:], ["ID"], ["ID3"])
    ts(T.I613[:], T.ID[:], 613.0, A.mult, ["ID"], ["I613"])
    ts(C("NI"), T.ID[:], -1.0, A.mult, ["ID"], ["NI"])
    ts(C("I2"), T.ID[:], 2.0, A.mult, ["ID"], ["I2"])
    ts(T.WB[:], T.BO[:, :, 0], q[:, 1:2], A.mult, ["BO", "q1"], ["WB"])
    fill(T.RM8[:], 1.0, ["RM8"])
    fill(T.KB0[:], 0.0, ["KB0"])
    fill(T.KB1[:], 0.0, ["KB1"])
    fill(T.RM[:, ::16], 0.0, ["RM"])
    fill(T.RM8[:, ::8], 0.0, ["RM8"])
    fill(T.MUL[:, 0:16], 256, ["MULa"])
    fill(T.MUL[:, 16:32], 1, ["MULb"])
    fill(T.MUL[:, 32:48], -1, ["MULc"])
    for k in range(16):
        ts(T.BK[:, k], T.BO[:], T.RA[:, k:k + 1], A.mult, ["BO", "RA"], ["BK%d" % k])

    def late_constants():
        for j, n in ((0, 0), (1, 2), (2, 3)):
            ts(T.AD[:, 16 * j:16 * j + 16], T.BS[:, 16 * j:16 * j + 16], q[:, n:n + 1], A.add,
               ["BS" + "abc"[j], "q%d" % n], ["AD" + "abc"[j]])

    def gather(e, out, win, off, R, W):
        if e == "V":
            op("V", R, W, [], lambda: v.tensor_copy(out, win.indirect(off)))
        else:
            op("S", R, W, [], lambda: s.activation(out, win.indirect(off), AF.Copy))

    def seats(t, c):
        n = str(c)
        if t == 0:
            copy(X("OFS", c)[:], T.S3[:, :, c, :], ["S3"], ["OFS" + n])
        else:
            key = "RZ%d%d" % (t - 1, c)
            ts(X("OFS", c)[:], T[key][:, :, 0:16], 0.0, A.add, [key, key + "o"], ["OFS" + n])

    def zrow(t, c):
        n = str(c)
        if t == 0:
            copy(X("ZC", c)[:], T.Z3[:, :, c, :], ["Z3"], ["ZC" + n])
        else:
            key = "RZ%d%d" % (t - 1, c)
            copy(X("ZC", c)[:], T[key][:, :, 16:32], [key, key + "o"], ["ZC" + n])
        Eb = X("E", c)
        op("P", ["ZC" + n, "BO"], [], ["E" + n], lambda: [
            p.matmul(Eb[:, 1], X("ZC", c)[:], T.BO[:], True, True),
            p.matmul(Eb[:, 2, :, 0], X("ZC", c)[:], T.BO[:, :, 0], True, True)])

    def part(name, c, a, b):
        return T[name][:, 2048 * c + 16 * a:2048 * c + 16 * b]

    def cgather(e, c, a, b):
        gather(e, part("CG", c, a, b), T.CW[:, 0:1024], X("OFS", c)[:, a:b], ["CW", "OFS%d" % c],
               ["CG%d%s" % (c, "b" if a else "a")])

    def mgather(e, c, a, b):
        gather(e, part("YG", c, a, b), T.MW[:, 0:1024], X("OFM", c)[:, a:b], ["MW", "OFM%d" % c],
               ["YG%d%s" % (c, "b" if a else "a")])

    def xgather(e, c):
        gather(e, fan("XG", c), T.XW[:, 0:4096], X("OFX", c)[:, 0:128], ["XW", "OFX%d" % c], ["XG%d" % c])

    def members(t, c):
        n = str(c)
        op("P", ["CG" + n + "a", "CG" + n + "b", "ID"], [], ["E" + n], lambda: [
            p.matmul(X("E", c)[:, 0, :, k], fan("CG", c, k, 16), T.ID[:, (k + t) & 15::16], True, True) for k in range(16)])

    def hashes(t, c):
        n = str(c)
        Eb, Qb, Lb = X("E", c), X("Q", c), X("L", c)
        es, eq, u1, wi, hi = X("ES", c), X("EQ", c), X("U1", c), X("WI", c), X("HI", c)
        EB = ["E" + n]
        copy(es[:], Eb[:, 0], [], ["ES" + n], EB)
        op("P", ["ES" + n, "ID"], [], ["L" + n], lambda: p.matmul(Lb[:, 0:128], es[:], T.ID[:], True, True))

        def base():
            r = [p.matmul(Qb[:, 0], T.ID[:], es[:], True, False)]
            if t > 0:
                r += [p.matmul(Qb[:, 0], T.ON2[:], X("O1", j)[:], False, False) for j in (0, 1)]
            return r
        op("P", ["ES" + n, "ID", "ON2", "O10", "O11"], [], ["Q" + n], base)
        ts(u1[:], Eb[:, 1], 1.0, A.add, [], ["U1" + n], EB)

        def equal(d):
            tt(eq[:, d - 1, :, d:16], es[:, :, d:16], Eb[:, 0, :, 0:16 - d], A.is_equal, ["ES" + n], ["EQ%d_%d" % (c, d)], EB)
            op("P", ["EQ%d_%d" % (c, d), "I613"], [], ["Q" + n],
               lambda: p.matmul(Qb[:, 0, :, d:16], T.I613[:], eq[:, d - 1, :, d:16], False, d == 15))
        equal(1)
        equal(2)
        copy(X("OFM", c)[:], Lb[:, 0:128], [], ["OFM" + n], ["L" + n])
        tt(wi[:], u1[:], Eb[:, 0], A.mult, ["U1" + n], ["WI" + n], EB)
        equal(3)
        equal(4)
        ts(wi[:], wi[:], 5, A.arith_shift_right, ["WI" + n], ["WI" + n])
        copy(K("UI", c, 0, 8), Eb[:, 2, :, 0], [], ["UIa" + n], EB)
        equal(5)
        equal(6)
        ts(K("UI", c, 8, 16), K("UI", c, 0, 8), 3, A.bitwise_and, ["UIa" + n], ["UIb" + n])
        equal(7)
        equal(8)
        ts(X("U3", c)[:], K("UI", c, 8, 16), 256.0, A.mult, ["UIb" + n], ["U3" + n])
        for d in range(9, 16):
            equal(d)
        copy(X("TT", c)[:, :, 0, :], es[:], ["ES" + n], ["TTa" + n])
        tt(hi[:], wi[:], Qb[:, 0], A.add, ["WI" + n], ["HI" + n], ["Q" + n])
        ts(hi[:], hi[:], 4095, A.bitwise_and, ["HI" + n], ["HI" + n])
        ts(X("HF", c)[:], hi[:], -2048.0, A.add, ["HI" + n], ["HF" + n])
        op("P", ["HF" + n, "ID"], [], ["L" + n], lambda: p.matmul(Lb[:, 0:128], X("HF", c)[:], T.ID[:], True, True))
        ts(X("H8", c)[:], hi[:], 8, A.arith_shift_right, ["HI" + n], ["H8" + n])
        ts(X("OFX", c)[:], Lb[:, 0:128], 2048.0, A.add, [], ["OFX" + n], ["L" + n])
        tt(K("VK", c), X("H8", c)[:], C("KC16"), A.add, ["H8" + n, "KC16"], ["VK" + n])

    def bins(c):
        n = str(c)
        op("P", ["XG" + n, "WB"], [], ["L" + n], lambda: [
            p.matmul(X("L", c)[:, 128 + k:256:16], fan("XG", c, k, 16), T.WB[:], True, True) for k in range(16)])

    def survivors(t, c):
        n = str(c)
        Lb, LB = X("L", c), ["L" + n]
        bi, ind = X("BI", c), X("IN", c)
        copy(bi[:], Lb[:, 128:256], [], ["BI" + n], LB)
        ts(bi[:], bi[:], 3, A.bitwise_and, ["BI" + n], ["BI" + n])
        ink = ["IN%d_%d" % (c, b) for b in range(4)]
        for b in range(4):
            ts(ind[:, 128 * b:128 * b + 128], bi[:], b, A.is_equal, ["BI" + n], [ink[b]], (), 4.0, A.mult)
        scan(X("CT", c)[:], T.RM[:], ind[:], 0.0, A.mult, A.add, ["RM"] + ink, ["CT" + n])
        tt(K("KI", c), X("CT", c)[:, 15::16], T.KCC[:], A.add, ["CT" + n, "KCC"], ["KI" + n])
        ts(K("KI", c), K("KI", c), 127, A.bitwise_and, ["KI" + n], ["KI" + n])
        tt(K("KJ", c, 0, 16), K("KI", c, 0, 16), K("KI", c, 16, 32), A.min, ["KI" + n], ["KJ" + n])
        tt(K("KJ", c, 16, 24), K("KJ", c, 0, 8), K("KJ", c, 8, 16), A.min, ["KJ" + n], ["KK" + n])
        ts(K("BN", c, 0, 8), K("KJ", c, 16, 24), 3, A.bitwise_and, ["KK" + n], ["BNa" + n])
        ts(K("BN", c, 8, 16), K("KJ", c, 16, 24), 2, A.arith_shift_right, ["KK" + n], ["BNb" + n])
        copy(X("KB", c)[:, ::16], K("BN", c), ["BNa" + n, "BNb" + n], ["KB" + n])
        scan(X("BB", c)[:], T.RM[:, 0:256], X("KB", c)[:], 0.0, A.mult, A.add, ["RM", "KB" + n], ["BB" + n])
        tt(K("SV", c), bi[:], X("BB", c)[:, 0:128], A.is_equal, ["BI" + n, "BB" + n], ["SV" + n])
        op("P", ["SV" + n, "ID"], [], LB, lambda: p.matmul(Lb[:, 0:128], K("SV", c), T.ID[:], True, True))
        scan(K("PR", c), T.RM[:, 0:128], K("SV", c), 0.0, A.mult, A.add, ["RM", "SV" + n], ["PR" + n])
        ts(K("AL", c), Lb[:, 0:128], -2.0, A.add, [], ["AL" + n], LB)

    def spread(c, ms):
        n = str(c)
        bks = ["BK%d" % k for k in range(16)]
        for m in ms:
            D, db = T["D%d" % (m & 1)], "D%d" % (m & 1)
            op("P", ["AL" + n] + bks, [], [db], lambda: [
                p.matmul(D[:, 128 * j:128 * j + 128], T.BK[:, 4 * m + j], K("AL", c), True, True) for j in range(4)])
            op("S", [], ["DS%d_%d" % (c, m)], [db], lambda: [
                s.activation(fan("DS", c, 4 * m + j, 16), D[:, 128 * j:128 * j + 128], AF.Copy) for j in range(4)])

    def ranks(c):
        n = str(c)
        Lb, LB, bb = X("L", c), ["L" + n], X("BB", c)
        op("P", ["PR" + n, "BB" + n, "ID", "NI", "I2", "KM7", "KM2"], [], LB, lambda: [
            p.matmul(Lb[:, 384:512], T.ID[:], bb[:, 128:256], True, False),
            p.matmul(Lb[:, 384:512], T.ID[:], C("KM7"), False, False),
            p.matmul(Lb[:, 384:512], C("NI"), K("PR", c), False, True),
            p.matmul(Lb[:, 256:384], C("NI"), bb[:, 128:256], True, False),
            p.matmul(Lb[:, 256:384], T.ID[:], C("KM2"), False, False),
            p.matmul(Lb[:, 256:384], C("I2"), K("PR", c), False, True)])

    def places(t, c):
        n = str(c)
        Lb, LB = X("L", c), ["L" + n]
        bb, TTb = X("BB", c), X("TT", c)
        tt(K("SVL", c), K("SV", c), K("VK", c), A.mult, ["SV" + n, "VK" + n], ["SVL" + n])
        if t < LEVELS - 1:
            ts(X("O1", c)[:], bb[:, 128:256], 0.0, A.is_equal, ["BB" + n], ["O1" + n])
        tt(K("TP", c), K("SV", c), Lb[:, 256:384], A.mult, ["SV" + n], ["TP" + n], LB)
        scan(K("VM", c), T.RM[:, 0:128], K("SVL", c), 0.0, A.mult, A.max, ["RM", "SVL" + n], ["VM" + n])
        tt(TTb[:, :, 1, :], K("TP", c), Lb[:, 384:512], A.add, ["TP" + n], ["TTb" + n], LB)
        tt(X("VT", c)[:], K("VM", c, 15, 128, 16), X("U3", c)[:], A.add, ["VM" + n, "U3" + n], ["VT" + n])
        tt(TTb[:, :, 2, :], TTb[:, :, 1, :], TTb[:, :, 1, :], A.mult, ["TTb" + n], ["TTc" + n])

    def turn(c):
        n = str(c)
        o = 128 + 64 * c
        op("P", ["VT" + n, "LS"], [], ["L0"], lambda: [
            p.matmul(T.L0[:, o + 8 * b:o + 8 * b + 8], T.LS[:, b], X("VT", c)[:], True, True) for b in range(8)])

    def lists():
        r = T.RL
        tt(T.LM[:], T.DG[:], T.L0[:, 128:256], A.mult, ["DG"], ["LM"], ["L0"])
        scan(T.LV[:], T.RM8[:], T.LM[:], 0.0, A.mult, A.add, ["RM8", "LM"], ["LV"])
        copy(T.VI[:], T.LV[:, 7::8], ["LV"], ["VI"])
        ts(r[:, 0:16], T.VI[:], 15, A.bitwise_and, ["VI"], ["Ra"])
        ts(r[:, 16:32], T.VI[:], 8, A.arith_shift_right, ["VI"], ["Rb"])
        ts(r[:, 32:48], T.VI[:], 4, A.arith_shift_right, ["VI"], ["Rc"], (), 15, A.bitwise_and)
        rr = ["Ra", "Rb", "Rc"]
        tt(r[:], r[:], T.MUL[:], A.mult, rr + ["MULa", "MULb", "MULc"], rr)
        tt(r[:], r[:], T.AD[:], A.add, rr + ["ADa", "ADb", "ADc"], rr)
        copy(T.LST[:], r[:], rr, ["LST"])

    def maximum(c, x):
        n = str(c)
        src = ["XG" + n] if x == "X" else ["YG" + n + "a", "YG" + n + "b"]
        scan(fan(x + "S", c), fan(x + "G", c), fan("DS", c), -1024.0, A.max, A.add,
             src + ["DS%d_%d" % (c, m) for m in range(4)], [x + "S" + n])

    def leave(t, c):
        n = str(c)
        xs, ys = fan("XS", c, 15, 16), fan("YS", c, 15, 16)
        if t == LEVELS - 1:
            ts(T.OS[:, :, c, :], ys, 1024.0, A.add, ["YS" + n], ["OS" + n])
            ts(T.OZ[:, :, c, :], xs, 1024.0, A.add, ["XS" + n], ["OZ" + n])
            return
        key = "%d%d" % (t, c)
        sz, rz = T["SZ" + key], T["RZ" + key]
        ts(sz[:, :, 0:16], ys, 1024.0, A.add, ["YS" + n], ["SZa" + key])
        ts(sz[:, :, 16:32], xs, 1024.0, A.add, ["XS" + n], ["SZb" + key])
        sync("G", ["SZa" + key, "SZb" + key], [], [])
        for call in calls_of(core, cores, topo):
            g.remote_dma_fused([RemoteDMATransfer(
                src=sz[:, cores.index(d), :], dst=rz[:, rank, :],
                dst_ids=[DstId(rid=topo.addr(d, core)[0], pnc=topo.addr(d, core)[1])],
                dma_engine_mask=sum(1 << e for e in en), remote_sem=T.sem["arr" + key]) for d, en in call],
                local_sem=T.sem["snt" + key])
        copy(rz[:, rank, :], sz[:, rank, :], ["SZa" + key, "SZb" + key], ["RZ" + key + "o"])
        total = sum(len(en) for o in cores if o != core for call in calls_of(o, cores, topo) for d, en in call if d == core)
        wr["RZ" + key] = ("arr" + key, total, {})

    def features(c):
        n = str(c)
        op("P", ["TTa" + n, "TTb" + n, "TTc" + n, "ID3"], [], ["E" + n], lambda: [
            p.matmul(X("E", c)[0:96, j], X("TT", c)[:, :, :, j::4], T.ID3[:], True, True) for j in range(4)])
        op("S", [], ["TL" + n], ["E" + n], lambda: s.activation(X("TL", c)[0:96], X("E", c)[0:96], AF.Copy))

    def pick(c, j):
        n = str(c)
        b, key = (X("E", c), "E" + n) if j & 1 else (X("Q", c), "Q" + n)
        op("P", ["TL" + n, "FQ"], [], [key], lambda: [
            p.matmul(b[:, i], T.FQ[0:96, i], X("TL", c)[0:96, j], True, True) for i in range(4)])
        op("S", ["q6"], ["FR%d_%d" % (c, j)], [key],
           lambda: s.activation(X("FR", c)[:, 4 * j:4 * j + 4], b[:], AF.Relu, bias=T.QC[:, 6:7]))

    def total(c, j):
        op("P", ["FR%d_%d" % (c, j), "ID"], [], ["E0"], lambda: [
            p.matmul(T.E0[:, c], T.ID[:], X("FR", c)[:, i], i == 0, i == 15) for i in range(4 * j, 4 * j + 4)])

    def cwrite():
        copy(T.FC[:], T.E0[:, 0:2], [], ["FC"], ["E0"])
        op("V", ["FC", "LST"], ["CW"], [], lambda: v.tensor_copy(T.CW[:, 0:1024].indirect(T.LST[:, 16:32]), T.FC[:]))

    def xnew():
        ts(T.NZ[:], T.XS[:, 15::16], 1024.0, A.add, ["XS0", "XS1"], ["NZ"])
        op("V", ["XG0", "XG1", "LST", "NZ"], ["XQ"], [], lambda: v.tensor_tensor(
            T.XQ[:], T.XG[:, 0:4096].indirect(T.LST[:, 32:48]), T.NZ[:], A.add))
        ts(T.XR[:], T.XQ[:], 1, A.arith_shift_right, ["XQ"], ["XR"])

    def xwrite():
        op("V", ["XR", "LST"], ["XW"], [], lambda: v.tensor_copy(T.XW[:, 0:4096].indirect(T.LST[:, 0:16]), T.XR[:]))

    def weights(a, b):
        iota(T.DI[:, a:b], [[1, b - a], [0, 128]], a + 1, 0, ["DI%d" % a])
        sel(T.DI[:, a:b], T.DI[:, a:b], [[0, b - a], [-1, 128]], A.is_equal, 0.0, 0, 1, ["DI%d" % a], ["DI%d" % a])

    for t in range(LEVELS):
        last = t == LEVELS - 1
        seats(t, 0)
        if t == 0:
            seats(t, 1)
            ts(T.CW[:], T.CM[:], 1023, A.bitwise_and, ["CM"], ["CW"])
        cgather("S", 0, 0, 64)
        cgather("V", 0, 64, 128)
        zrow(t, 0)
        if t > 0:
            seats(t, 1)
        cgather("S", 1, 0, 64)
        cgather("S", 1, 64, 128)
        zrow(t, 1)
        if t == 0:
            ts(T.MW[:], T.CM[:], 10, A.arith_shift_right, ["CM"], ["MW"])
        else:
            xnew()
        members(t, 0)
        hashes(t, 0)
        mgather("S", 0, 0, 64)
        if t == 0:
            late_constants()
        else:
            xwrite()
        members(t, 1)
        xgather("S", 0)
        hashes(t, 1)
        xgather("S", 1)
        mgather("S", 1, 0, 64)
        bins(0)
        bins(1)
        survivors(t, 0)
        ranks(0)
        spread(0, (0, 1, 2, 3))
        places(t, 0)
        features(0)
        for j in range(4):
            pick(0, j)
        mgather("V", 0, 64, 128)
        mgather("S", 1, 64, 128)
        survivors(t, 1)
        ranks(1)
        spread(1, (0, 1))
        places(t, 1)
        features(1)
        turn(0)
        turn(1)
        spread(1, (2, 3))
        for j in range(4):
            total(0, j)
        pick(1, 0)
        pick(1, 1)
        total(1, 0)
        pick(1, 2)
        total(1, 1)
        pick(1, 3)
        total(1, 2)
        total(1, 3)
        maximum(0, "X")
        maximum(0, "Y")
        leave(t, 0)
        maximum(1, "X")
        maximum(1, "Y")
        leave(t, 1)
        if not last:
            weights(32 * t, 32 * t + 16)
            weights(32 * t + 16, 32 * t + 32)
        lists()
        if last:
            xnew()
            xwrite()
        cwrite()
    dma("Y", "os", T.ys[:], T.OS[:], ["OS0", "OS1"], [])
    dma("Y", "oz", T.yz[:], T.OZ[:], ["OZ0", "OZ1"], [])
    dis = ["DI0", "DI16", "DI32", "DI48"]
    op("P", ["XW"] + dis, [], ["L0"], lambda: [
        p.matmul(T.L0[:, 0:64], T.DI[:, m], T.XW[:, 64 * m:64 * m + 64], m == 0, m == 63) for m in range(64)])
    copy(T.CF[:], T.CW[:], ["CW"], ["CF"])
    op("P", ["CF"] + dis, [], ["L1"], lambda: [
        p.matmul(T.L1[:, 0:64], T.DI[:, m], T.CF[:, 64 * m:64 * m + 64], m == 0, m == 15) for m in range(16)])
    copy(T.OX[:], T.L0[:, 0:64], [], ["OX"], ["L0"])
    dma("Y", "ox", T.yx[:], T.OX[:], ["OX"], [])
    copy(T.OC[:], T.L1[:, 0:64], [], ["OC"], ["L1"])
    dma("Y", "oc", T.yc[:], T.OC[:], ["OC"], [])
    for sem in sorted(cnt):
        g.wait_ge(T.sem[sem], cnt[sem])
    for t in range(LEVELS - 1):
        for c in (0, 1):
            g.wait_ge(T.sem["snt%d%d" % (t, c)], sum(len(en) for call in calls_of(core, cores, topo) for d, en in call))
